import numpy as np
import ml_dtypes


def mxq(x, axis, fmt="e4m3"):
    dtype, down = {"e4m3": (ml_dtypes.float8_e4m3fn, 7), "e5m2": (ml_dtypes.float8_e5m2, 14)}[fmt]
    v = np.moveaxis(np.asarray(x, np.float32).astype(ml_dtypes.bfloat16).astype(np.float64), axis, -1)
    blocks = v.reshape(v.shape[:-1] + (-1, 32))
    amax = np.abs(blocks).max(-1, keepdims=True)
    byte = np.maximum(np.where(amax > 0, np.frexp(amax)[1] - 1 + 127, 0) - down, 1)
    scale = np.exp2(byte - 127.0)
    codes = (blocks / scale).astype(np.float32).astype(dtype).astype(np.float64)
    return np.moveaxis((codes * scale).reshape(v.shape), -1, axis)


WIDE = False


def mx_kscale(k):
    if not WIDE:
        return np.ones(k)
    levels = np.array([10, -10, 5, -5, 0])
    if k % 512:
        return np.exp2(np.random.permutation(np.resize(levels, k // 32))).repeat(32)
    a = np.empty((k // 512, 16))
    for p in range(k // 512):
        a[p, :8] = np.random.permutation(np.resize(levels, 8))
        for g in range(8):
            far = levels[np.abs(levels - a[p, g]) >= 10]
            a[p, g + 8] = far[np.random.randint(len(far))]
    return np.exp2(a.ravel()).repeat(32)


def f64(x):
    return np.asarray(x).astype(np.float64)


def striped(idx):
    return np.tile(idx.reshape(-1, 16).T, (8, 1)).astype(np.uint16)


def unstriped(offs):
    return offs[:16].T.reshape(-1).astype(np.int64)


E2M1 = np.array([0.0, 0.5, 1.0, 1.5, 2.0, 3.0, 4.0, 6.0, -0.0, -0.5, -1.0, -1.5, -2.0, -3.0, -4.0, -6.0])


def pack_weight(w, fmt):
    k, n = w.shape
    w = f64(np.asarray(w, np.float32).astype(ml_dtypes.bfloat16)).reshape(k // 32, 32, n)
    amax = np.abs(w).max(1)
    if fmt == "e4m3":
        byte = np.frexp(amax)[1] - 1 + 127 - 7
    else:
        mant, ex = np.frexp(amax / 6.0)
        byte = np.where(mant > 0.5, ex, ex - 1) + 127
    byte = np.clip(np.where(amax > 0, byte, 1), 1, 254)
    scaled = (w * np.exp2(127.0 - byte)[:, None, :]).reshape(k, n).astype(np.float32)
    by_word = np.ascontiguousarray(scaled.reshape(k // 512, 128, 4, n).transpose(0, 1, 3, 2))
    if fmt == "e4m3":
        words = by_word.astype(ml_dtypes.float8_e4m3fn).view(np.uint8)
    else:
        c = by_word.astype(ml_dtypes.float4_e2m1fn).view(np.uint8) & 0xF
        words = (c[..., 0::2] | (c[..., 1::2] << 4)).reshape(k // 512, 128, 2 * n)
    return np.ascontiguousarray(words), np.ascontiguousarray(byte.astype(np.uint8).reshape(k // 512, 16, n))


def unpack_weight(words, scales, fmt):
    g, _, n = scales.shape
    words = np.ascontiguousarray(words).reshape(g, 128, n, -1)
    if fmt == "e4m3":
        vals = words.view(ml_dtypes.float8_e4m3fn).astype(np.float64)
    else:
        nib = np.empty((g, 128, n, 4), np.uint8)
        nib[..., 0::2] = words & 0xF
        nib[..., 1::2] = words >> 4
        vals = E2M1[nib]
    vals = vals * np.repeat(np.exp2(scales.astype(np.float64) - 127.0), 8, axis=1)[..., None]
    return vals.transpose(0, 1, 3, 2).reshape(g * 512, n)


def relu2(v):
    return np.maximum(v, 0.0) ** 2


K, T, E, B, H, N = 512, 768, 8, 6, 512, 256


def setup_inputs():
    n = np.random.standard_normal
    s = mx_kscale(K)
    u = mx_kscale(H)
    slot_token = np.random.permutation(T)[:128 * B]
    block = np.sort(np.random.randint(E, size=B))
    x = pack_weight(n((K, T)) * s[:, None], "e4m3")
    w1 = pack_weight(n((K, E * H)) / np.sqrt(K) / s[:, None] * np.tile(u, E), "e4m3")
    w2 = pack_weight(n((H, E * N)) / np.sqrt(H) / u[:, None] ** 2, "e4m3")
    return {
        "x_words": x[0],
        "x_scales": x[1],
        "w1_words": w1[0],
        "w1_scales": w1[1],
        "w2_words": w2[0],
        "w2_scales": w2[1],
        "gate": (np.tile(np.random.uniform(0.2, 1.0, 128 * B), (128, 1))).astype(np.float32),
        "offs": striped(slot_token),
        "offs2": striped((block[:, None] * H + np.arange(H)).reshape(-1)),
        "offs3": striped((block[:, None] * N + np.arange(N)).reshape(-1)),
    }


def reference(x_words, x_scales, w1_words, w1_scales, w2_words, w2_scales, gate, offs, offs2, offs3):
    idx, idx2, idx3 = unstriped(offs), unstriped(offs2), unstriped(offs3)
    xq = unpack_weight(x_words, x_scales, "e4m3")[:, idx]
    w1 = unpack_weight(w1_words, w1_scales, "e4m3")[:, idx2]
    w2 = unpack_weight(w2_words, w2_scales, "e4m3")[:, idx3]
    h = np.concatenate([w1[:, m * H:(m + 1) * H].T @ xq[:, 128 * m:128 * m + 128] for m in range(B)], axis=1)
    hq = mxq(relu2(h), 0, "e4m3")
    y = np.concatenate([w2[:, m * N:(m + 1) * N].T @ hq[:, 128 * m:128 * m + 128] for m in range(B)], axis=1)
    out = np.zeros((N, T))
    out[:, idx] = f64(gate[:1]) * y
    return out

@@ -1,0 +1,149 @@
+from contextlib import ExitStack
+
+import concourse.mybir as mybir
+from concourse.masks import make_identity
+
+K, T, E, B, H, N = 512, 768, 8, 6, 512, 256
+FLOPS = 2 * B * 128 * (K * H + H * N)
+
+F32 = mybir.dt.float32
+BF16 = mybir.dt.bfloat16
+I32 = mybir.dt.int32
+U32 = mybir.dt.uint32
+U16 = mybir.dt.uint16
+U8 = mybir.dt.uint8
+FP8X4 = mybir.dt.float8_e4m3fn_x4
+ACT = mybir.ActivationFunctionType
+MULT = mybir.AluOpType.mult
+
+P = 128
+S = B * P
+LIST_ROWS = 16
+TOKEN_WINDOW = 1024
+
+
+def tile_moe_dyn_relu2_kernel(
+    tc, x_words, x_scales, w1_words, w1_scales, w2_words, w2_scales, gate, offs, offs2, offs3, out
+):
+    nc = tc.nc
+    with ExitStack() as ctx:
+        lists = ctx.enter_context(tc.tile_pool(name="lists", bufs=1))
+        keep = ctx.enter_context(tc.tile_pool(name="keep", bufs=1))
+        ring = ctx.enter_context(tc.tile_pool(name="ring", bufs=2))
+        psum = ctx.enter_context(tc.psum_pool(name="psum", bufs=2))
+
+        def entries(lst, lo, hi):
+            return lst[:, lo // LIST_ROWS : hi // LIST_ROWS]
+
+        def load_words(queue, dst, src):
+            queue.dma_start(out=dst, in_=src[0].rearrange("p n t -> p (n t)").bitcast(I32))
+
+        def load_scales(dst, src):
+            rows = src[0].rearrange("(q r) n -> r q n", r=4)
+            for r in range(4):
+                nc.scalar.dma_start(out=dst[r:P:32, : src.shape[2]].bitcast(I32), in_=rows[r].bitcast(I32))
+
+        tok = lists.tile([P, S // LIST_ROWS], U16, name="tok")
+        col1 = lists.tile([P, B * H // LIST_ROWS], U16, name="col1")
+        col2 = lists.tile([P, B * N // LIST_ROWS], U16, name="col2")
+        xw = keep.tile([P, TOKEN_WINDOW], I32, name="xw")
+        xs = keep.tile([P, TOKEN_WINDOW], U8, name="xs")
+        w1w = keep.tile([P, E * H], I32, name="w1w")
+        w1s = keep.tile([P, E * H], U8, name="w1s")
+        w2w = keep.tile([P, E * N], I32, name="w2w")
+        w2s = keep.tile([P, E * N], U8, name="w2s")
+        g = keep.tile([P, S], F32, name="g")
+        ident = keep.tile([P, P], F32, name="ident")
+
+        nc.vector.memset(w1s[:].bitcast(I32), 0)
+        nc.vector.memset(xs[:].bitcast(I32), 0)
+        nc.vector.memset(w2s[:].bitcast(I32), 0)
+        nc.vector.memset(xw[:, T:], 0)
+        make_identity(nc, ident[:])
+
+        nc.sync.dma_start(tok[:], offs)
+        load_words(nc.sync, xw[:, :T], x_words)
+        nc.sync.dma_start(col2[:], offs3)
+        load_words(nc.sync, w2w[:], w2_words)
+        nc.sync.dma_start(col1[:], offs2)
+        load_scales(w1s, w1_scales)
+        load_words(nc.sync, w1w[:], w1_words)
+        load_scales(xs, x_scales)
+        load_scales(w2s, w2_scales)
+        nc.sync.dma_start(out=g[:], in_=gate)
+
+        xg = keep.tile([P, S], U32, name="xg", align_bytes=64)
+        xgs = keep.tile([P, S], U8, name="xgs", align_bytes=64)
+        w1gs = keep.tile([P, B * H], U8, name="w1gs", align_bytes=64)
+        w2g = keep.tile([P, B * N], U32, name="w2g", align_bytes=64)
+
+        nc.vector.tensor_copy(xg[:], xw[:].bitcast(U32).indirect(tok[:]))
+        nc.vector.tensor_copy(w2g[:], w2w[:].bitcast(U32).indirect(col2[:]))
+        half1 = B * H // 2
+        for lo in (0, half1):
+            nc.vector.tensor_copy(w1gs[:, lo : lo + half1], w1s[:].indirect(entries(col1, lo, lo + half1)))
+        nc.vector.tensor_copy(xgs[:], xs[:].indirect(tok[:]))
+
+        hb_a = keep.tile([P, 4 * H], BF16, name="hb_a", tag="slot_b", align_bytes=64)
+        hb_b = keep.tile([P, 2 * H], BF16, name="hb_b", align_bytes=64)
+
+        def hidden(m):
+            return hb_a[:, m * H : (m + 1) * H] if m < 4 else hb_b[:, (m - 4) * H : (m - 3) * H]
+
+        for pair in range(B // 2):
+            w1g = keep.tile([P, 2 * H], U32, name="w1g", tag="w1g%d" % pair, align_bytes=64)
+            lo = pair * 2 * H
+            nc.vector.tensor_copy(w1g[:], w1w[:].bitcast(U32).indirect(entries(col1, lo, lo + 2 * H)))
+            for j in range(2):
+                m = 2 * pair + j
+                pre = psum.tile([P, H], F32, name="pre")
+                nc.tensor.matmul_mx(
+                    out=pre[:],
+                    lhsT=xg[:, m * P : (m + 1) * P].bitcast(FP8X4),
+                    lhsT_scale=xgs[:, m * P : (m + 1) * P],
+                    rhs=w1g[:, j * H : (j + 1) * H].bitcast(FP8X4),
+                    rhs_scale=w1gs[:, m * H : (m + 1) * H],
+                    start=True,
+                    stop=True,
+                )
+                pos = ring.tile([P, 4, P], F32, name="pos")
+                nc.scalar.activation(pos[:], pre[:].rearrange("u (p t) -> u t p", t=4), ACT.Relu)
+                turned = psum.tile([P, 4, P], F32, name="turned")
+                for t in range(4):
+                    nc.tensor.transpose(turned[:, t, :], pos[:, t, :], ident[:])
+                nc.scalar.activation(
+                    hidden(m).rearrange("p (u t) -> p u t", t=4), turned[:].rearrange("p t u -> p u t"), ACT.Square
+                )
+
+        hq = keep.tile([P, S], U32, name="hq", align_bytes=64)
+        hqs = keep.tile([P, S], U8, name="hqs", align_bytes=64)
+        half2 = B * N // 2
+        w2gs_a = keep.tile([P, half2], U8, name="w2gs_a", tag="w1g0", align_bytes=64)
+        nc.vector.tensor_copy(w2gs_a[:], w2s[:].indirect(entries(col2, 0, half2)))
+        nc.vector.quantize_mx(out=hq[:, : 4 * P].bitcast(FP8X4), scales=hqs[:, : 4 * P], in_=hb_a[:])
+        w2gs_b = keep.tile([P, half2], U8, name="w2gs_b", tag="slot_b", align_bytes=64)
+        nc.vector.tensor_copy(w2gs_b[:], w2s[:].indirect(entries(col2, half2, 2 * half2)))
+        nc.vector.quantize_mx(out=hq[:, 4 * P :].bitcast(FP8X4), scales=hqs[:, 4 * P :], in_=hb_b[:])
+
+        res = [keep.tile([P, T], F32, name="res%d" % c) for c in range(2)]
+        for h in range(2):
+            y = ring.tile([P, 2, S // 2], F32, name="y")
+            for j in range(B // 2):
+                m = h * (B // 2) + j
+                acc = psum.tile([P, 2, P], F32, name="acc")
+                for c in range(2):
+                    nc.tensor.matmul_mx(
+                        out=acc[:, c, :],
+                        lhsT=w2g[:, m * N + c * P : m * N + (c + 1) * P].bitcast(FP8X4),
+                        lhsT_scale=(w2gs_a, w2gs_b)[h][:, j * N + c * P : j * N + (c + 1) * P],
+                        rhs=hq[:, m * P : (m + 1) * P].bitcast(FP8X4),
+                        rhs_scale=hqs[:, m * P : (m + 1) * P],
+                        start=True,
+                        stop=True,
+                    )
+                nc.scalar.copy(y[:, :, j * P : (j + 1) * P], acc[:])
+            lo, hi = h * S // 2, (h + 1) * S // 2
+            for c in range(2):
+                nc.vector.tensor_tensor(res[c][:].indirect(entries(tok, lo, hi)), y[:, c, :], g[:, lo:hi], MULT)
+        for c in range(2):
+            nc.sync.dma_start(out=out[c * P : (c + 1) * P, :], in_=res[c][:])

@@ -20,6 +20,7 @@ P = 128
 S = B * P
 LIST_ROWS = 16
 TOKEN_WINDOW = 1024
+ROW0 = P - 16
 
 
 def tile_moe_dyn_relu2_kernel(
@@ -38,62 +39,75 @@ def tile_moe_dyn_relu2_kernel(
         def load_words(queue, dst, src):
             queue.dma_start(out=dst, in_=src[0].rearrange("p n t -> p (n t)").bitcast(I32))
 
-        def load_scales(dst, src):
-            rows = src[0].rearrange("(q r) n -> r q n", r=4)
-            for r in range(4):
-                nc.scalar.dma_start(out=dst[r:P:32, : src.shape[2]].bitcast(I32), in_=rows[r].bitcast(I32))
+        def quadrant_rows(plane, r):
+            return plane[r:P:32, :].bitcast(I32)
 
         tok = lists.tile([P, S // LIST_ROWS], U16, name="tok")
         col1 = lists.tile([P, B * H // LIST_ROWS], U16, name="col1")
         col2 = lists.tile([P, B * N // LIST_ROWS], U16, name="col2")
-        xw = keep.tile([P, TOKEN_WINDOW], I32, name="xw")
-        xs = keep.tile([P, TOKEN_WINDOW], U8, name="xs")
+        xw = keep.tile([P, TOKEN_WINDOW], I32, name="xw", tag="xw_then_w2w")
+        xs = keep.tile([P, T], U8, name="xs")
         w1w = keep.tile([P, E * H], I32, name="w1w")
         w1s = keep.tile([P, E * H], U8, name="w1s")
-        w2w = keep.tile([P, E * N], I32, name="w2w")
-        w2s = keep.tile([P, E * N], U8, name="w2s")
-        g = keep.tile([P, S], F32, name="g")
+        w2s = keep.tile([P, E * N], U8, name="w2s", tag="w2s_then_gate")
         ident = keep.tile([P, P], F32, name="ident")
+        xg = keep.tile([P, S], U32, name="xg", align_bytes=64)
+        xgs_rows = keep.tile([P, S], U8, name="xgs_rows")
+        xgs = keep.tile([P, S], U8, name="xgs", align_bytes=64)
+        w1gs = keep.tile([P, B * H], U8, name="w1gs", align_bytes=64)
+        w2g = keep.tile([P, B * N], U32, name="w2g", align_bytes=64)
+        w2gs_rows = keep.tile([P, B * N], U8, name="w2gs_rows")
+        w2gs = keep.tile([P, B * N], U8, name="w2gs", align_bytes=64)
 
         nc.vector.memset(w1s[:].bitcast(I32), 0)
-        nc.vector.memset(xs[:].bitcast(I32), 0)
-        nc.vector.memset(w2s[:].bitcast(I32), 0)
         nc.vector.memset(xw[:, T:], 0)
+        nc.vector.memset(xs[:ROW0, :].bitcast(I32), 0)
+        nc.vector.memset(w2s[:ROW0, :].bitcast(I32), 0)
+        nc.gpsimd.memset(xgs[:].bitcast(I32), 0)
+        nc.gpsimd.memset(w2gs[:].bitcast(I32), 0)
         make_identity(nc, ident[:])
 
         nc.sync.dma_start(tok[:], offs)
         load_words(nc.sync, xw[:, :T], x_words)
+        nc.sync.dma_start(out=xs[ROW0:, :].bitcast(I32), in_=x_scales[0].bitcast(I32))
         nc.sync.dma_start(col2[:], offs3)
-        load_words(nc.sync, w2w[:], w2_words)
+        nc.sync.dma_start(out=w2s[ROW0:, :].bitcast(I32), in_=w2_scales[0].bitcast(I32))
         nc.sync.dma_start(col1[:], offs2)
-        load_scales(w1s, w1_scales)
         load_words(nc.sync, w1w[:], w1_words)
-        load_scales(xs, x_scales)
-        load_scales(w2s, w2_scales)
-        nc.sync.dma_start(out=g[:], in_=gate)
-
-        xg = keep.tile([P, S], U32, name="xg", align_bytes=64)
-        xgs = keep.tile([P, S], U8, name="xgs", align_bytes=64)
-        w1gs = keep.tile([P, B * H], U8, name="w1gs", align_bytes=64)
-        w2g = keep.tile([P, B * N], U32, name="w2g", align_bytes=64)
+        w1_rows = w1_scales[0].rearrange("(q r) n -> r q n", r=4)
+        for r in range(4):
+            nc.sync.dma_start(out=quadrant_rows(w1s, r), in_=w1_rows[r].bitcast(I32))
 
         nc.vector.tensor_copy(xg[:], xw[:].bitcast(U32).indirect(tok[:]))
-        nc.vector.tensor_copy(w2g[:], w2w[:].bitcast(U32).indirect(col2[:]))
-        half1 = B * H // 2
-        for lo in (0, half1):
-            nc.vector.tensor_copy(w1gs[:, lo : lo + half1], w1s[:].indirect(entries(col1, lo, lo + half1)))
-        nc.vector.tensor_copy(xgs[:], xs[:].indirect(tok[:]))
+        w2w = keep.tile([P, E * N], I32, name="w2w", tag="xw_then_w2w")
+        load_words(nc.sync, w2w[:], w2_words)
+        half = S // 2
+        for lo in (0, half):
+            nc.vector.tensor_copy(xgs_rows[:, lo : lo + half], xs[:].indirect(entries(tok, lo, lo + half)))
+        for r in range(4):
+            nc.scalar.dma_start(out=quadrant_rows(xgs, r), in_=xgs_rows[ROW0 + r : P : 4, :].bitcast(I32))
+        nc.vector.tensor_copy(w2gs_rows[:], w2s[:].indirect(col2[:]))
+        g = keep.tile([P, S], F32, name="g", tag="w2s_then_gate")
+        nc.sync.dma_start(out=g[:], in_=gate)
+        for r in range(4):
+            nc.sync.dma_start(out=quadrant_rows(w2gs, r), in_=w2gs_rows[ROW0 + r : P : 4, :].bitcast(I32))
 
-        hb_a = keep.tile([P, 4 * H], BF16, name="hb_a", tag="slot_b", align_bytes=64)
-        hb_b = keep.tile([P, 2 * H], BF16, name="hb_b", align_bytes=64)
+        hq = keep.tile([P, S], U32, name="hq", align_bytes=64)
+        hqs = keep.tile([P, S], U8, name="hqs", align_bytes=64)
+        y = [keep.tile([P, S], F32, name="y%d" % c) for c in range(2)]
+        hb = [keep.tile([P, 2 * H], BF16, name="hb%d" % q, tag="hb%d" % q, align_bytes=64) for q in range(3)]
 
-        def hidden(m):
-            return hb_a[:, m * H : (m + 1) * H] if m < 4 else hb_b[:, (m - 4) * H : (m - 3) * H]
-
-        for pair in range(B // 2):
-            w1g = keep.tile([P, 2 * H], U32, name="w1g", tag="w1g%d" % pair, align_bytes=64)
+        def gather_w1_words(pair, tag):
+            w1g = keep.tile([P, 2 * H], U32, name="w1g", tag=tag, align_bytes=64)
             lo = pair * 2 * H
             nc.vector.tensor_copy(w1g[:], w1w[:].bitcast(U32).indirect(entries(col1, lo, lo + 2 * H)))
+            return w1g
+
+        def gather_w1_scales(pair):
+            lo = pair * 2 * H
+            nc.vector.tensor_copy(w1gs[:, lo : lo + 2 * H], w1s[:].indirect(entries(col1, lo, lo + 2 * H)))
+
+        def first_layer(pair, w1g):
             for j in range(2):
                 m = 2 * pair + j
                 pre = psum.tile([P, H], F32, name="pre")
@@ -112,38 +126,50 @@ def tile_moe_dyn_relu2_kernel(
                 for t in range(4):
                     nc.tensor.transpose(turned[:, t, :], pos[:, t, :], ident[:])
                 nc.scalar.activation(
-                    hidden(m).rearrange("p (u t) -> p u t", t=4), turned[:].rearrange("p t u -> p u t"), ACT.Square
+                    hb[pair][:, j * H : (j + 1) * H].rearrange("p (u t) -> p u t", t=4),
+                    turned[:].rearrange("p t u -> p u t"),
+                    ACT.Square,
                 )
 
-        hq = keep.tile([P, S], U32, name="hq", align_bytes=64)
-        hqs = keep.tile([P, S], U8, name="hqs", align_bytes=64)
-        half2 = B * N // 2
-        w2gs_a = keep.tile([P, half2], U8, name="w2gs_a", tag="w1g0", align_bytes=64)
-        nc.vector.tensor_copy(w2gs_a[:], w2s[:].indirect(entries(col2, 0, half2)))
-        nc.vector.quantize_mx(out=hq[:, : 4 * P].bitcast(FP8X4), scales=hqs[:, : 4 * P], in_=hb_a[:])
-        w2gs_b = keep.tile([P, half2], U8, name="w2gs_b", tag="slot_b", align_bytes=64)
-        nc.vector.tensor_copy(w2gs_b[:], w2s[:].indirect(entries(col2, half2, 2 * half2)))
-        nc.vector.quantize_mx(out=hq[:, 4 * P :].bitcast(FP8X4), scales=hqs[:, 4 * P :], in_=hb_b[:])
-
-        res = [keep.tile([P, T], F32, name="res%d" % c) for c in range(2)]
-        for h in range(2):
-            y = ring.tile([P, 2, S // 2], F32, name="y")
-            for j in range(B // 2):
-                m = h * (B // 2) + j
-                acc = psum.tile([P, 2, P], F32, name="acc")
-                for c in range(2):
+        def second_layer(pair):
+            slots = slice(pair * 2 * P, (pair + 1) * 2 * P)
+            nc.vector.quantize_mx(out=hq[:, slots].bitcast(FP8X4), scales=hqs[:, slots], in_=hb[pair][:])
+            for c in range(2):
+                acc = psum.tile([P, 2 * P], F32, name="acc%d" % c)
+                for j in range(2):
+                    m = 2 * pair + j
+                    cols = slice(m * N + c * P, m * N + (c + 1) * P)
                     nc.tensor.matmul_mx(
-                        out=acc[:, c, :],
-                        lhsT=w2g[:, m * N + c * P : m * N + (c + 1) * P].bitcast(FP8X4),
-                        lhsT_scale=(w2gs_a, w2gs_b)[h][:, j * N + c * P : j * N + (c + 1) * P],
+                        out=acc[:, j * P : (j + 1) * P],
+                        lhsT=w2g[:, cols].bitcast(FP8X4),
+                        lhsT_scale=w2gs[:, cols],
                         rhs=hq[:, m * P : (m + 1) * P].bitcast(FP8X4),
                         rhs_scale=hqs[:, m * P : (m + 1) * P],
                         start=True,
                         stop=True,
                     )
-                nc.scalar.copy(y[:, :, j * P : (j + 1) * P], acc[:])
-            lo, hi = h * S // 2, (h + 1) * S // 2
-            for c in range(2):
-                nc.vector.tensor_tensor(res[c][:].indirect(entries(tok, lo, hi)), y[:, c, :], g[:, lo:hi], MULT)
-        for c in range(2):
-            nc.sync.dma_start(out=out[c * P : (c + 1) * P, :], in_=res[c][:])
+                nc.scalar.copy(y[c][:, slots], acc[:])
+
+        def scatter(res, c, lo, hi):
+            nc.vector.tensor_tensor(res[:].indirect(entries(tok, lo, hi)), y[c][:, lo:hi], g[:, lo:hi], MULT)
+
+        for pair in range(2):
+            w1g = gather_w1_words(pair, "w1g")
+            gather_w1_scales(pair)
+            first_layer(pair, w1g)
+        gather_w1_scales(2)
+        nc.vector.tensor_copy(w2g[:], w2w[:].bitcast(U32).indirect(col2[:]))
+        second_layer(0)
+        w1g = gather_w1_words(2, "hb0")
+        second_layer(1)
+        first_layer(2, w1g)
+        res0 = keep.tile([P, T], F32, name="res0", tag="hb1", align_bytes=64)
+        scatter(res0, 0, 0, 2 * P)
+        scatter(res0, 0, 2 * P, 4 * P)
+        second_layer(2)
+        res1 = keep.tile([P, TOKEN_WINDOW], F32, name="res1", tag="hb2", align_bytes=64)
+        scatter(res1, 1, 0, 4 * P)
+        scatter(res0, 0, 4 * P, S)
+        nc.sync.dma_start(out=out[:P, :], in_=res0[:])
+        scatter(res1, 1, 4 * P, S)
+        nc.sync.dma_start(out=out[P:, :], in_=res1[:, :T])

@@ -20,7 +20,6 @@ P = 128
 S = B * P
 LIST_ROWS = 16
 TOKEN_WINDOW = 1024
-ROW0 = P - 16
 
 
 def tile_moe_dyn_relu2_kernel(
@@ -30,119 +29,99 @@ def tile_moe_dyn_relu2_kernel(
     with ExitStack() as ctx:
         lists = ctx.enter_context(tc.tile_pool(name="lists", bufs=1))
         keep = ctx.enter_context(tc.tile_pool(name="keep", bufs=1))
-        ring = ctx.enter_context(tc.tile_pool(name="ring", bufs=2))
-        psum = ctx.enter_context(tc.psum_pool(name="psum", bufs=2))
+        ring = ctx.enter_context(tc.tile_pool(name="ring", bufs=3))
+        psum3 = ctx.enter_context(tc.psum_pool(name="psum3", bufs=3))
+        psum1 = ctx.enter_context(tc.psum_pool(name="psum1", bufs=1))
 
         def entries(lst, lo, hi):
             return lst[:, lo // LIST_ROWS : hi // LIST_ROWS]
 
-        def load_words(queue, dst, src):
-            queue.dma_start(out=dst, in_=src[0].rearrange("p n t -> p (n t)").bitcast(I32))
+        def load_words(dst, src):
+            nc.sync.dma_start(out=dst, in_=src[0].rearrange("p n t -> p (n t)").bitcast(I32))
 
-        def quadrant_rows(plane, r):
-            return plane[r:P:32, :].bitcast(I32)
+        def load_scales(plane, src, width):
+            rows = src[0].rearrange("(q r) n -> r q n", r=4)
+            for r in range(4):
+                nc.sync.dma_start(out=plane[r:P:32, :width].bitcast(I32), in_=rows[r].bitcast(I32))
 
         tok = lists.tile([P, S // LIST_ROWS], U16, name="tok")
         col1 = lists.tile([P, B * H // LIST_ROWS], U16, name="col1")
         col2 = lists.tile([P, B * N // LIST_ROWS], U16, name="col2")
-        xw = keep.tile([P, TOKEN_WINDOW], I32, name="xw", tag="xw_then_w2w")
-        xs = keep.tile([P, T], U8, name="xs")
+        xw = keep.tile([P, TOKEN_WINDOW], I32, name="xw")
+        xs = keep.tile([P, TOKEN_WINDOW], U8, name="xs")
         w1w = keep.tile([P, E * H], I32, name="w1w")
         w1s = keep.tile([P, E * H], U8, name="w1s")
-        w2s = keep.tile([P, E * N], U8, name="w2s", tag="w2s_then_gate")
+        w2w = keep.tile([P, E * N], I32, name="w2w")
+        w2s = keep.tile([P, E * N], U8, name="w2s")
+        g = keep.tile([P, S], F32, name="g")
         ident = keep.tile([P, P], F32, name="ident")
         xg = keep.tile([P, S], U32, name="xg", align_bytes=64)
-        xgs_rows = keep.tile([P, S], U8, name="xgs_rows")
         xgs = keep.tile([P, S], U8, name="xgs", align_bytes=64)
-        w1gs = keep.tile([P, B * H], U8, name="w1gs", align_bytes=64)
-        w2g = keep.tile([P, B * N], U32, name="w2g", align_bytes=64)
-        w2gs_rows = keep.tile([P, B * N], U8, name="w2gs_rows")
         w2gs = keep.tile([P, B * N], U8, name="w2gs", align_bytes=64)
-
-        nc.vector.memset(w1s[:].bitcast(I32), 0)
-        nc.vector.memset(xw[:, T:], 0)
-        nc.vector.memset(xs[:ROW0, :].bitcast(I32), 0)
-        nc.vector.memset(w2s[:ROW0, :].bitcast(I32), 0)
-        nc.gpsimd.memset(xgs[:].bitcast(I32), 0)
-        nc.gpsimd.memset(w2gs[:].bitcast(I32), 0)
-        make_identity(nc, ident[:])
-
-        nc.sync.dma_start(tok[:], offs)
-        load_words(nc.sync, xw[:, :T], x_words)
-        nc.sync.dma_start(out=xs[ROW0:, :].bitcast(I32), in_=x_scales[0].bitcast(I32))
-        nc.sync.dma_start(col2[:], offs3)
-        nc.sync.dma_start(out=w2s[ROW0:, :].bitcast(I32), in_=w2_scales[0].bitcast(I32))
-        nc.sync.dma_start(col1[:], offs2)
-        load_words(nc.sync, w1w[:], w1_words)
-        w1_rows = w1_scales[0].rearrange("(q r) n -> r q n", r=4)
-        for r in range(4):
-            nc.sync.dma_start(out=quadrant_rows(w1s, r), in_=w1_rows[r].bitcast(I32))
-
-        nc.vector.tensor_copy(xg[:], xw[:].bitcast(U32).indirect(tok[:]))
-        w2w = keep.tile([P, E * N], I32, name="w2w", tag="xw_then_w2w")
-        load_words(nc.sync, w2w[:], w2_words)
-        half = S // 2
-        for lo in (0, half):
-            nc.vector.tensor_copy(xgs_rows[:, lo : lo + half], xs[:].indirect(entries(tok, lo, lo + half)))
-        for r in range(4):
-            nc.scalar.dma_start(out=quadrant_rows(xgs, r), in_=xgs_rows[ROW0 + r : P : 4, :].bitcast(I32))
-        nc.vector.tensor_copy(w2gs_rows[:], w2s[:].indirect(col2[:]))
-        g = keep.tile([P, S], F32, name="g", tag="w2s_then_gate")
-        nc.sync.dma_start(out=g[:], in_=gate)
-        for r in range(4):
-            nc.sync.dma_start(out=quadrant_rows(w2gs, r), in_=w2gs_rows[ROW0 + r : P : 4, :].bitcast(I32))
-
         hq = keep.tile([P, S], U32, name="hq", align_bytes=64)
         hqs = keep.tile([P, S], U8, name="hqs", align_bytes=64)
         y = [keep.tile([P, S], F32, name="y%d" % c) for c in range(2)]
         hb = [keep.tile([P, 2 * H], BF16, name="hb%d" % q, tag="hb%d" % q, align_bytes=64) for q in range(3)]
 
-        def gather_w1_words(pair, tag):
-            w1g = keep.tile([P, 2 * H], U32, name="w1g", tag=tag, align_bytes=64)
-            lo = pair * 2 * H
-            nc.vector.tensor_copy(w1g[:], w1w[:].bitcast(U32).indirect(entries(col1, lo, lo + 2 * H)))
-            return w1g
+        nc.vector.memset(xs[:].bitcast(I32), 0)
+        nc.vector.memset(w1s[:].bitcast(I32), 0)
+        nc.vector.memset(xw[:, T:], 0)
+        nc.vector.memset(w2s[:].bitcast(I32), 0)
+        make_identity(nc, ident[:])
 
-        def gather_w1_scales(pair):
-            lo = pair * 2 * H
-            nc.vector.tensor_copy(w1gs[:, lo : lo + 2 * H], w1s[:].indirect(entries(col1, lo, lo + 2 * H)))
+        nc.sync.dma_start(tok[:], offs)
+        load_scales(xs, x_scales, T)
+        load_words(xw[:, :T], x_words)
+        nc.sync.dma_start(col1[:], offs2)
+        load_scales(w1s, w1_scales, E * H)
+        load_words(w1w[:], w1_words)
+        nc.sync.dma_start(col2[:], offs3)
+        load_scales(w2s, w2_scales, E * N)
+        load_words(w2w[:], w2_words)
+        nc.sync.dma_start(out=g[:], in_=gate)
 
-        def first_layer(pair, w1g):
-            for j in range(2):
-                m = 2 * pair + j
-                pre = psum.tile([P, H], F32, name="pre")
-                nc.tensor.matmul_mx(
-                    out=pre[:],
-                    lhsT=xg[:, m * P : (m + 1) * P].bitcast(FP8X4),
-                    lhsT_scale=xgs[:, m * P : (m + 1) * P],
-                    rhs=w1g[:, j * H : (j + 1) * H].bitcast(FP8X4),
-                    rhs_scale=w1gs[:, m * H : (m + 1) * H],
-                    start=True,
-                    stop=True,
-                )
-                pos = ring.tile([P, 4, P], F32, name="pos")
-                nc.scalar.activation(pos[:], pre[:].rearrange("u (p t) -> u t p", t=4), ACT.Relu)
-                turned = psum.tile([P, 4, P], F32, name="turned")
-                for t in range(4):
-                    nc.tensor.transpose(turned[:, t, :], pos[:, t, :], ident[:])
-                nc.scalar.activation(
-                    hb[pair][:, j * H : (j + 1) * H].rearrange("p (u t) -> p u t", t=4),
-                    turned[:].rearrange("p t u -> p u t"),
-                    ACT.Square,
-                )
+        def gather(name, window, lst, width, lo, hi, dtype, tag=None):
+            dst = keep.tile([P, (hi - lo) * width], dtype, name=name, tag=tag or name, align_bytes=64)
+            nc.vector.tensor_copy(dst[:], window.indirect(entries(lst, lo * width, hi * width)))
+            return [dst[:, j * width : (j + 1) * width] for j in range(hi - lo)]
 
-        def second_layer(pair):
+        def first_layer(m, words, scales):
+            pre = psum3.tile([P, H], F32, name="pre")
+            nc.tensor.matmul_mx(
+                out=pre[:],
+                lhsT=xg[:, m * P : (m + 1) * P].bitcast(FP8X4),
+                lhsT_scale=xgs[:, m * P : (m + 1) * P],
+                rhs=words.bitcast(FP8X4),
+                rhs_scale=scales,
+                start=True,
+                stop=True,
+            )
+            pos = ring.tile([P, 4, P], F32, name="pos")
+            nc.scalar.activation(pos[:], pre[:].rearrange("u (p t) -> u t p", t=4), ACT.Relu)
+            turned = psum3.tile([P, 4, P], F32, name="turned")
+            for t in range(4):
+                nc.tensor.transpose(turned[:, t, :], pos[:, t, :], ident[:])
+            j = m % 2
+            nc.scalar.activation(
+                hb[m // 2][:, j * H : (j + 1) * H].rearrange("p (u t) -> p u t", t=4),
+                turned[:].rearrange("p t u -> p u t"),
+                ACT.Square,
+            )
+
+        def quantise(pair):
             slots = slice(pair * 2 * P, (pair + 1) * 2 * P)
             nc.vector.quantize_mx(out=hq[:, slots].bitcast(FP8X4), scales=hqs[:, slots], in_=hb[pair][:])
+
+        def second_layer(pair, w2g):
+            slots = slice(pair * 2 * P, (pair + 1) * 2 * P)
             for c in range(2):
-                acc = psum.tile([P, 2 * P], F32, name="acc%d" % c)
+                acc = psum1.tile([P, 2 * P], F32, name="acc%d" % c)
                 for j in range(2):
                     m = 2 * pair + j
-                    cols = slice(m * N + c * P, m * N + (c + 1) * P)
                     nc.tensor.matmul_mx(
                         out=acc[:, j * P : (j + 1) * P],
-                        lhsT=w2g[:, cols].bitcast(FP8X4),
-                        lhsT_scale=w2gs[:, cols],
+                        lhsT=w2g[m][:, c * P : (c + 1) * P].bitcast(FP8X4),
+                        lhsT_scale=w2gs[:, m * N + c * P : m * N + (c + 1) * P],
                         rhs=hq[:, m * P : (m + 1) * P].bitcast(FP8X4),
                         rhs_scale=hqs[:, m * P : (m + 1) * P],
                         start=True,
@@ -153,20 +132,34 @@ def tile_moe_dyn_relu2_kernel(
         def scatter(res, c, lo, hi):
             nc.vector.tensor_tensor(res[:].indirect(entries(tok, lo, hi)), y[c][:, lo:hi], g[:, lo:hi], MULT)
 
-        for pair in range(2):
-            w1g = gather_w1_words(pair, "w1g")
-            gather_w1_scales(pair)
-            first_layer(pair, w1g)
-        gather_w1_scales(2)
-        nc.vector.tensor_copy(w2g[:], w2w[:].bitcast(U32).indirect(col2[:]))
-        second_layer(0)
-        w1g = gather_w1_words(2, "hb0")
-        second_layer(1)
-        first_layer(2, w1g)
+        w1_window = w1w[:].bitcast(U32)
+        w2_window = w2w[:].bitcast(U32)
+        nc.vector.tensor_copy(xgs[:], xs[:].indirect(tok[:]))
+        nc.vector.tensor_copy(xg[:], xw[:].bitcast(U32).indirect(tok[:]))
+        w1gs = gather("w1gs_a", w1s[:], col1, H, 0, 4, U8)
+        w1g = gather("w1g0", w1_window, col1, H, 0, 1, U32)
+        first_layer(0, w1g[0], w1gs[0])
+        w1g = w1g + gather("w1g1", w1_window, col1, H, 1, 2, U32)
+        first_layer(1, w1g[1], w1gs[1])
+        w1g = w1g + gather("w1g23", w1_window, col1, H, 2, 4, U32)
+        first_layer(2, w1g[2], w1gs[2])
+        first_layer(3, w1g[3], w1gs[3])
+        w1g = w1g + gather("w1g45", w1_window, col1, H, 4, 6, U32)
+        w1gs = w1gs + gather("w1gs_b", w1s[:], col1, H, 4, 6, U8, tag="w1g0")
+        nc.vector.tensor_copy(w2gs[:], w2s[:].indirect(col2[:]))
+        w2g = gather("w2g01", w2_window, col2, N, 0, 2, U32)
+        quantise(0)
+        w2g = w2g + gather("w2g_rest", w2_window, col2, N, 2, 6, U32, tag="hb0")
+        second_layer(0, w2g)
+        first_layer(4, w1g[4], w1gs[4])
+        quantise(1)
+        second_layer(1, w2g)
+        first_layer(5, w1g[5], w1gs[5])
         res0 = keep.tile([P, T], F32, name="res0", tag="hb1", align_bytes=64)
         scatter(res0, 0, 0, 2 * P)
         scatter(res0, 0, 2 * P, 4 * P)
-        second_layer(2)
+        quantise(2)
+        second_layer(2, w2g)
         res1 = keep.tile([P, TOKEN_WINDOW], F32, name="res1", tag="hb2", align_bytes=64)
         scatter(res1, 1, 0, 4 * P)
         scatter(res0, 0, 4 * P, S)

@@ -20,6 +20,7 @@ P = 128
 S = B * P
 LIST_ROWS = 16
 TOKEN_WINDOW = 1024
+ROW0 = P - 16
 
 
 def tile_moe_dyn_relu2_kernel(
@@ -39,51 +40,63 @@ def tile_moe_dyn_relu2_kernel(
         def load_words(dst, src):
             nc.sync.dma_start(out=dst, in_=src[0].rearrange("p n t -> p (n t)").bitcast(I32))
 
-        def load_scales(plane, src, width):
+        def quadrant_rows(plane, r):
+            return plane[r:P:32, :].bitcast(I32)
+
+        def load_scales(plane, src):
             rows = src[0].rearrange("(q r) n -> r q n", r=4)
             for r in range(4):
-                nc.sync.dma_start(out=plane[r:P:32, :width].bitcast(I32), in_=rows[r].bitcast(I32))
+                nc.sync.dma_start(out=quadrant_rows(plane, r), in_=rows[r].bitcast(I32))
 
         tok = lists.tile([P, S // LIST_ROWS], U16, name="tok")
         col1 = lists.tile([P, B * H // LIST_ROWS], U16, name="col1")
         col2 = lists.tile([P, B * N // LIST_ROWS], U16, name="col2")
         xw = keep.tile([P, TOKEN_WINDOW], I32, name="xw")
+        w2w = keep.tile([P, E * N], I32, name="w2w")
+        g = keep.tile([P, S], F32, name="g")
         xs = keep.tile([P, TOKEN_WINDOW], U8, name="xs")
         w1w = keep.tile([P, E * H], I32, name="w1w")
         w1s = keep.tile([P, E * H], U8, name="w1s")
-        w2w = keep.tile([P, E * N], I32, name="w2w")
         w2s = keep.tile([P, E * N], U8, name="w2s")
-        g = keep.tile([P, S], F32, name="g")
         ident = keep.tile([P, P], F32, name="ident")
         xg = keep.tile([P, S], U32, name="xg", align_bytes=64)
+        xgs_rows = keep.tile([P, S], U8, name="xgs_rows")
         xgs = keep.tile([P, S], U8, name="xgs", align_bytes=64)
-        w2gs = keep.tile([P, B * N], U8, name="w2gs", align_bytes=64)
-        hq = keep.tile([P, S], U32, name="hq", align_bytes=64)
         hqs = keep.tile([P, S], U8, name="hqs", align_bytes=64)
-        y = [keep.tile([P, S], F32, name="y%d" % c) for c in range(2)]
-        hb = [keep.tile([P, 2 * H], BF16, name="hb%d" % q, tag="hb%d" % q, align_bytes=64) for q in range(3)]
+        hb01 = keep.tile([P, 2 * H], BF16, name="hb01", align_bytes=64)
+        hb23 = keep.tile([P, 2 * H], BF16, name="hb23", align_bytes=64)
+        hb4 = keep.tile([P, H], BF16, name="hb4", align_bytes=64)
+        hb5 = keep.tile([P, H], BF16, name="hb5", align_bytes=64)
+        hb = [hb01[:, :H], hb01[:, H:], hb23[:, :H], hb23[:, H:], hb4[:], hb5[:]]
+        y = {}
+        res = [keep.tile([P, T], F32, name="res%d" % c) for c in range(2)]
 
-        nc.vector.memset(xs[:].bitcast(I32), 0)
         nc.vector.memset(w1s[:].bitcast(I32), 0)
+        nc.vector.memset(xs[:ROW0, :T].bitcast(I32), 0)
+        nc.vector.memset(xs[:, T:].bitcast(I32), 0)
         nc.vector.memset(xw[:, T:], 0)
         nc.vector.memset(w2s[:].bitcast(I32), 0)
+        nc.vector.memset(xgs[:].bitcast(I32), 0)
         make_identity(nc, ident[:])
 
         nc.sync.dma_start(tok[:], offs)
-        load_scales(xs, x_scales, T)
-        load_words(xw[:, :T], x_words)
+        nc.sync.dma_start(out=xs[ROW0:, :T].bitcast(I32), in_=x_scales[0].bitcast(I32))
         nc.sync.dma_start(col1[:], offs2)
-        load_scales(w1s, w1_scales, E * H)
+        load_words(xw[:, :T], x_words)
+        load_scales(w1s, w1_scales)
         load_words(w1w[:], w1_words)
-        nc.sync.dma_start(col2[:], offs3)
-        load_scales(w2s, w2_scales, E * N)
-        load_words(w2w[:], w2_words)
-        nc.sync.dma_start(out=g[:], in_=gate)
 
-        def gather(name, window, lst, width, lo, hi, dtype, tag=None):
-            dst = keep.tile([P, (hi - lo) * width], dtype, name=name, tag=tag or name, align_bytes=64)
+        def gather(dst, window, lst, width, lo, hi):
             nc.vector.tensor_copy(dst[:], window.indirect(entries(lst, lo * width, hi * width)))
             return [dst[:, j * width : (j + 1) * width] for j in range(hi - lo)]
+
+        def gather_w1(name, window, dtype, lo, hi, tag=None):
+            dst = keep.tile([P, (hi - lo) * H], dtype, name=name, tag=tag or name, align_bytes=64)
+            return gather(dst, window, col1, H, lo, hi)
+
+        def gather_w2(name, window, dtype, lo, hi, tag=None):
+            dst = keep.tile([P, (hi - lo) * N], dtype, name=name, tag=tag or name, align_bytes=64)
+            return gather(dst, window, col2, N, lo, hi)
 
         def first_layer(m, words, scales):
             pre = psum3.tile([P, H], F32, name="pre")
@@ -97,72 +110,90 @@ def tile_moe_dyn_relu2_kernel(
                 stop=True,
             )
             pos = ring.tile([P, 4, P], F32, name="pos")
-            nc.scalar.activation(pos[:], pre[:].rearrange("u (p t) -> u t p", t=4), ACT.Relu)
+            nc.scalar.activation(
+                pos[:].rearrange("u t p -> u p t"), pre[:].rearrange("u (p t) -> u p t", t=4), ACT.Relu
+            )
             turned = psum3.tile([P, 4, P], F32, name="turned")
             for t in range(4):
                 nc.tensor.transpose(turned[:, t, :], pos[:, t, :], ident[:])
-            j = m % 2
             nc.scalar.activation(
-                hb[m // 2][:, j * H : (j + 1) * H].rearrange("p (u t) -> p u t", t=4),
+                hb[m].rearrange("p (u t) -> p u t", t=4),
                 turned[:].rearrange("p t u -> p u t"),
                 ACT.Square,
             )
 
-        def quantise(pair):
-            slots = slice(pair * 2 * P, (pair + 1) * 2 * P)
-            nc.vector.quantize_mx(out=hq[:, slots].bitcast(FP8X4), scales=hqs[:, slots], in_=hb[pair][:])
+        def quantise(lo, hi, src, tag):
+            hq = keep.tile([P, (hi - lo) * P], U32, name="hq%d" % lo, tag=tag, align_bytes=64)
+            nc.vector.quantize_mx(out=hq[:].bitcast(FP8X4), scales=hqs[:, lo * P : hi * P], in_=src[:])
+            return hq
 
-        def second_layer(pair, w2g):
-            slots = slice(pair * 2 * P, (pair + 1) * 2 * P)
+        def second_layer(lo, hi, hq, cuts=(1, 1)):
             for c in range(2):
-                acc = psum1.tile([P, 2 * P], F32, name="acc%d" % c)
-                for j in range(2):
-                    m = 2 * pair + j
+                acc = psum1.tile([P, (hi - lo) * P], F32, name="acc%d" % c)
+                for m in range(lo, hi):
+                    scales, words = w2gs[m], w2g[m]
+                    cols = slice((m - lo) * P, (m - lo + 1) * P)
                     nc.tensor.matmul_mx(
-                        out=acc[:, j * P : (j + 1) * P],
-                        lhsT=w2g[m][:, c * P : (c + 1) * P].bitcast(FP8X4),
-                        lhsT_scale=w2gs[:, m * N + c * P : m * N + (c + 1) * P],
-                        rhs=hq[:, m * P : (m + 1) * P].bitcast(FP8X4),
+                        out=acc[:, cols],
+                        lhsT=words[:, c * P : (c + 1) * P].bitcast(FP8X4),
+                        lhsT_scale=scales[:, c * P : (c + 1) * P],
+                        rhs=hq[:, cols].bitcast(FP8X4),
                         rhs_scale=hqs[:, m * P : (m + 1) * P],
                         start=True,
                         stop=True,
                     )
-                nc.scalar.copy(y[c][:, slots], acc[:])
+                width = (hi - lo) // cuts[c]
+                for m in range(lo, hi, width):
+                    y[m, c] = keep.tile([P, width * P], F32, name="y%d_%d" % (m, c), align_bytes=64)
+                    nc.scalar.copy(y[m, c][:], acc[:, (m - lo) * P : (m - lo + width) * P])
 
-        def scatter(res, c, lo, hi):
-            nc.vector.tensor_tensor(res[:].indirect(entries(tok, lo, hi)), y[c][:, lo:hi], g[:, lo:hi], MULT)
+        def scatter(c, lo, hi):
+            window = res[c][:].indirect(entries(tok, lo * P, hi * P))
+            nc.vector.tensor_tensor(window, y[lo, c][:], g[:, lo * P : hi * P], MULT)
 
         w1_window = w1w[:].bitcast(U32)
-        w2_window = w2w[:].bitcast(U32)
-        nc.vector.tensor_copy(xgs[:], xs[:].indirect(tok[:]))
+        nc.vector.tensor_copy(xgs_rows[:], xs[:].indirect(tok[:]))
+        for r in range(4):
+            nc.sync.dma_start(out=quadrant_rows(xgs, r), in_=xgs_rows[ROW0 + r : P : 4, :].bitcast(I32))
+        nc.sync.dma_start(col2[:], offs3)
+        load_scales(w2s, w2_scales)
+        load_words(w2w[:], w2_words)
+        nc.sync.dma_start(out=g[:], in_=gate)
         nc.vector.tensor_copy(xg[:], xw[:].bitcast(U32).indirect(tok[:]))
-        w1gs = gather("w1gs_a", w1s[:], col1, H, 0, 4, U8)
-        w1g = gather("w1g0", w1_window, col1, H, 0, 1, U32)
-        first_layer(0, w1g[0], w1gs[0])
-        w1g = w1g + gather("w1g1", w1_window, col1, H, 1, 2, U32)
-        first_layer(1, w1g[1], w1gs[1])
-        w1g = w1g + gather("w1g23", w1_window, col1, H, 2, 4, U32)
+        w1gs = gather_w1("w1gs_a", w1s[:], U8, 0, 4)
+        w1g = []
+        for m in range(2):
+            w1g = w1g + gather_w1("w1g%d" % m, w1_window, U32, m, m + 1)
+            first_layer(m, w1g[m], w1gs[m])
+        w1g = w1g + gather_w1("w1g23", w1_window, U32, 2, 4)
         first_layer(2, w1g[2], w1gs[2])
         first_layer(3, w1g[3], w1gs[3])
-        w1g = w1g + gather("w1g45", w1_window, col1, H, 4, 6, U32)
-        w1gs = w1gs + gather("w1gs_b", w1s[:], col1, H, 4, 6, U8, tag="w1g0")
-        nc.vector.tensor_copy(w2gs[:], w2s[:].indirect(col2[:]))
-        w2g = gather("w2g01", w2_window, col2, N, 0, 2, U32)
-        quantise(0)
-        w2g = w2g + gather("w2g_rest", w2_window, col2, N, 2, 6, U32, tag="hb0")
-        second_layer(0, w2g)
+        w1gs = w1gs + gather_w1("w1gs_b", w1s[:], U8, 4, 6, tag="w1g0")
+        w1g = w1g + gather_w1("w1g45", w1_window, U32, 4, 6)
+        w2_window = w2w[:].bitcast(U32)
+        w2gs = gather_w2("w2gs", w2s[:], U8, 0, B)
+        w2g = gather_w2("w2g01", w2_window, U32, 0, 2)
+        hq = quantise(0, 2, hb01, "hq0")
+        w2g.extend(gather_w2("w2g_rest", w2_window, U32, 2, B, tag="hb01"))
+        second_layer(0, 2, hq, (2, 1))
         first_layer(4, w1g[4], w1gs[4])
-        quantise(1)
-        second_layer(1, w2g)
+        scatter(0, 0, 1)
+        scatter(0, 1, 2)
+        hq = quantise(2, 4, hb23, "y0_0")
+        second_layer(2, 4, hq, (2, 2))
+        scatter(1, 0, 2)
         first_layer(5, w1g[5], w1gs[5])
-        res0 = keep.tile([P, T], F32, name="res0", tag="hb1", align_bytes=64)
-        scatter(res0, 0, 0, 2 * P)
-        scatter(res0, 0, 2 * P, 4 * P)
-        quantise(2)
-        second_layer(2, w2g)
-        res1 = keep.tile([P, TOKEN_WINDOW], F32, name="res1", tag="hb2", align_bytes=64)
-        scatter(res1, 1, 0, 4 * P)
-        scatter(res0, 0, 4 * P, S)
-        nc.sync.dma_start(out=out[:P, :], in_=res0[:])
-        scatter(res1, 1, 4 * P, S)
-        nc.sync.dma_start(out=out[P:, :], in_=res1[:, :T])
+        scatter(0, 2, 3)
+        scatter(0, 3, 4)
+        hq = quantise(4, 5, hb4, "y2_0")
+        second_layer(4, 5, hq)
+        scatter(1, 2, 3)
+        scatter(1, 3, 4)
+        hq = quantise(5, 6, hb5, "y2_1")
+        second_layer(5, 6, hq)
+        scatter(0, 4, 5)
+        scatter(1, 4, 5)
+        scatter(0, 5, 6)
+        nc.sync.dma_start(out=out[:P, :], in_=res[0][:])
+        scatter(1, 5, 6)
+        nc.sync.dma_start(out=out[P:, :], in_=res[1][:])

@@ -32,7 +32,7 @@ def tile_moe_dyn_relu2_kernel(
         keep = ctx.enter_context(tc.tile_pool(name="keep", bufs=1))
         ring = ctx.enter_context(tc.tile_pool(name="ring", bufs=3))
         psum3 = ctx.enter_context(tc.psum_pool(name="psum3", bufs=3))
-        psum1 = ctx.enter_context(tc.psum_pool(name="psum1", bufs=1))
+        psum2 = ctx.enter_context(tc.psum_pool(name="psum2", bufs=2))
 
         def entries(lst, lo, hi):
             return lst[:, lo // LIST_ROWS : hi // LIST_ROWS]
@@ -66,8 +66,7 @@ def tile_moe_dyn_relu2_kernel(
         hb01 = keep.tile([P, 2 * H], BF16, name="hb01", align_bytes=64)
         hb23 = keep.tile([P, 2 * H], BF16, name="hb23", align_bytes=64)
         hb4 = keep.tile([P, H], BF16, name="hb4", align_bytes=64)
-        hb5 = keep.tile([P, H], BF16, name="hb5", align_bytes=64)
-        hb = [hb01[:, :H], hb01[:, H:], hb23[:, :H], hb23[:, H:], hb4[:], hb5[:]]
+        hb = [hb01[:, :H], hb01[:, H:], hb23[:, :H], hb23[:, H:], hb4[:]]
         y = {}
         res = [keep.tile([P, T], F32, name="res%d" % c) for c in range(2)]
 
@@ -127,29 +126,31 @@ def tile_moe_dyn_relu2_kernel(
             nc.vector.quantize_mx(out=hq[:].bitcast(FP8X4), scales=hqs[:, lo * P : hi * P], in_=src[:])
             return hq
 
-        def second_layer(lo, hi, hq, cuts=(1, 1)):
+        def second_layer(m, hq, cols, apart):
+            acc = psum2.tile([P, 2, P], F32, name="acc")
             for c in range(2):
-                acc = psum1.tile([P, (hi - lo) * P], F32, name="acc%d" % c)
-                for m in range(lo, hi):
-                    scales, words = w2gs[m], w2g[m]
-                    cols = slice((m - lo) * P, (m - lo + 1) * P)
-                    nc.tensor.matmul_mx(
-                        out=acc[:, cols],
-                        lhsT=words[:, c * P : (c + 1) * P].bitcast(FP8X4),
-                        lhsT_scale=scales[:, c * P : (c + 1) * P],
-                        rhs=hq[:, cols].bitcast(FP8X4),
-                        rhs_scale=hqs[:, m * P : (m + 1) * P],
-                        start=True,
-                        stop=True,
-                    )
-                width = (hi - lo) // cuts[c]
-                for m in range(lo, hi, width):
-                    y[m, c] = keep.tile([P, width * P], F32, name="y%d_%d" % (m, c), align_bytes=64)
-                    nc.scalar.copy(y[m, c][:], acc[:, (m - lo) * P : (m - lo + width) * P])
+                nc.tensor.matmul_mx(
+                    out=acc[:, c, :],
+                    lhsT=w2g[m][:, c * P : (c + 1) * P].bitcast(FP8X4),
+                    lhsT_scale=w2gs[m][:, c * P : (c + 1) * P],
+                    rhs=hq[:, cols].bitcast(FP8X4),
+                    rhs_scale=hqs[:, m * P : (m + 1) * P],
+                    start=True,
+                    stop=True,
+                )
+            if apart:
+                for c in range(2):
+                    half = keep.tile([P, P], F32, name="y%d_%d" % (m, c), align_bytes=64)
+                    nc.scalar.copy(half[:], acc[:, c, :])
+                    y[m, c] = half[:]
+            else:
+                both = keep.tile([P, 2, P], F32, name="y%d" % m)
+                nc.scalar.copy(both[:], acc[:])
+                y[m, 0], y[m, 1] = both[:, 0, :], both[:, 1, :]
 
-        def scatter(c, lo, hi):
-            window = res[c][:].indirect(entries(tok, lo * P, hi * P))
-            nc.vector.tensor_tensor(window, y[lo, c][:], g[:, lo * P : hi * P], MULT)
+        def scatter(m, c):
+            window = res[c][:].indirect(entries(tok, m * P, (m + 1) * P))
+            nc.vector.tensor_tensor(window, y[m, c], g[:, m * P : (m + 1) * P], MULT)
 
         w1_window = w1w[:].bitcast(U32)
         nc.vector.tensor_copy(xgs_rows[:], xs[:].indirect(tok[:]))
@@ -160,7 +161,7 @@ def tile_moe_dyn_relu2_kernel(
         load_words(w2w[:], w2_words)
         nc.sync.dma_start(out=g[:], in_=gate)
         nc.vector.tensor_copy(xg[:], xw[:].bitcast(U32).indirect(tok[:]))
-        w1gs = gather_w1("w1gs_a", w1s[:], U8, 0, 4)
+        w1gs = gather_w1("w1gs012", w1s[:], U8, 0, 3) + gather_w1("w1gs34", w1s[:], U8, 3, 5)
         w1g = []
         for m in range(2):
             w1g = w1g + gather_w1("w1g%d" % m, w1_window, U32, m, m + 1)
@@ -168,32 +169,38 @@ def tile_moe_dyn_relu2_kernel(
         w1g = w1g + gather_w1("w1g23", w1_window, U32, 2, 4)
         first_layer(2, w1g[2], w1gs[2])
         first_layer(3, w1g[3], w1gs[3])
-        w1gs = w1gs + gather_w1("w1gs_b", w1s[:], U8, 4, 6, tag="w1g0")
+        w1gs = w1gs + gather_w1("w1gs5", w1s[:], U8, 5, 6, tag="w1g0")
         w1g = w1g + gather_w1("w1g45", w1_window, U32, 4, 6)
         w2_window = w2w[:].bitcast(U32)
         w2gs = gather_w2("w2gs", w2s[:], U8, 0, B)
         w2g = gather_w2("w2g01", w2_window, U32, 0, 2)
         hq = quantise(0, 2, hb01, "hq0")
         w2g.extend(gather_w2("w2g_rest", w2_window, U32, 2, B, tag="hb01"))
-        second_layer(0, 2, hq, (2, 1))
+        first, second = slice(0, P), slice(P, 2 * P)
+        second_layer(0, hq, first, True)
+        second_layer(1, hq, second, False)
         first_layer(4, w1g[4], w1gs[4])
-        scatter(0, 0, 1)
-        scatter(0, 1, 2)
+        scatter(0, 0)
+        scatter(0, 1)
         hq = quantise(2, 4, hb23, "y0_0")
-        second_layer(2, 4, hq, (2, 2))
-        scatter(1, 0, 2)
+        second_layer(2, hq, first, True)
+        second_layer(3, hq, second, True)
+        hb5 = keep.tile([P, H], BF16, name="hb5", tag="y0_0", align_bytes=64)
+        hb.append(hb5[:])
         first_layer(5, w1g[5], w1gs[5])
-        scatter(0, 2, 3)
-        scatter(0, 3, 4)
+        scatter(1, 0)
+        scatter(1, 1)
+        scatter(2, 0)
+        scatter(2, 1)
         hq = quantise(4, 5, hb4, "y2_0")
-        second_layer(4, 5, hq)
-        scatter(1, 2, 3)
-        scatter(1, 3, 4)
-        hq = quantise(5, 6, hb5, "y2_1")
-        second_layer(5, 6, hq)
-        scatter(0, 4, 5)
-        scatter(1, 4, 5)
-        scatter(0, 5, 6)
+        second_layer(4, hq, first, False)
+        scatter(3, 0)
+        scatter(3, 1)
+        hq = quantise(5, 6, hb5, "y3_0")
+        second_layer(5, hq, first, False)
+        scatter(4, 0)
+        scatter(4, 1)
+        scatter(5, 0)
         nc.sync.dma_start(out=out[:P, :], in_=res[0][:])
-        scatter(1, 5, 6)
+        scatter(5, 1)
         nc.sync.dma_start(out=out[P:, :], in_=res[1][:])

@@ -20,6 +20,9 @@ P = 128
 S = B * P
 LIST_ROWS = 16
 TOKEN_WINDOW = 1024
+PRE_BANK = "ABABAB"
+TURNED_BANK = "CDEFGD"
+ACC_BANK = ("FG", "HH", "EE", "CC", "AA", "BB")
 ROW0 = P - 16
 
 
@@ -30,9 +33,8 @@ def tile_moe_dyn_relu2_kernel(
     with ExitStack() as ctx:
         lists = ctx.enter_context(tc.tile_pool(name="lists", bufs=1))
         keep = ctx.enter_context(tc.tile_pool(name="keep", bufs=1))
-        ring = ctx.enter_context(tc.tile_pool(name="ring", bufs=3))
-        psum3 = ctx.enter_context(tc.psum_pool(name="psum3", bufs=3))
-        psum2 = ctx.enter_context(tc.psum_pool(name="psum2", bufs=2))
+        ring = ctx.enter_context(tc.tile_pool(name="ring", bufs=2))
+        psum = ctx.enter_context(tc.psum_pool(name="psum", bufs=1))
 
         def entries(lst, lo, hi):
             return lst[:, lo // LIST_ROWS : hi // LIST_ROWS]
@@ -43,9 +45,9 @@ def tile_moe_dyn_relu2_kernel(
         def quadrant_rows(plane, r):
             return plane[r:P:32, :].bitcast(I32)
 
-        def load_scales(plane, src):
+        def load_scales(plane, src, lo=0, hi=4):
             rows = src[0].rearrange("(q r) n -> r q n", r=4)
-            for r in range(4):
+            for r in range(lo, hi):
                 nc.sync.dma_start(out=quadrant_rows(plane, r), in_=rows[r].bitcast(I32))
 
         tok = lists.tile([P, S // LIST_ROWS], U16, name="tok")
@@ -57,16 +59,13 @@ def tile_moe_dyn_relu2_kernel(
         xs = keep.tile([P, TOKEN_WINDOW], U8, name="xs")
         w1w = keep.tile([P, E * H], I32, name="w1w")
         w1s = keep.tile([P, E * H], U8, name="w1s")
-        w2s = keep.tile([P, E * N], U8, name="w2s")
+        w2s = keep.tile([P, E * N], U8, name="w2s", align_bytes=64)
         ident = keep.tile([P, P], F32, name="ident")
         xg = keep.tile([P, S], U32, name="xg", align_bytes=64)
         xgs_rows = keep.tile([P, S], U8, name="xgs_rows")
         xgs = keep.tile([P, S], U8, name="xgs", align_bytes=64)
         hqs = keep.tile([P, S], U8, name="hqs", align_bytes=64)
-        hb01 = keep.tile([P, 2 * H], BF16, name="hb01", align_bytes=64)
-        hb23 = keep.tile([P, 2 * H], BF16, name="hb23", align_bytes=64)
-        hb4 = keep.tile([P, H], BF16, name="hb4", align_bytes=64)
-        hb = [hb01[:, :H], hb01[:, H:], hb23[:, :H], hb23[:, H:], hb4[:]]
+        hb = [keep.tile([P, H], BF16, name="hb%d" % m, align_bytes=64) for m in range(B)]
         y = {}
         res = [keep.tile([P, T], F32, name="res%d" % c) for c in range(2)]
 
@@ -98,7 +97,7 @@ def tile_moe_dyn_relu2_kernel(
             return gather(dst, window, col2, N, lo, hi)
 
         def first_layer(m, words, scales):
-            pre = psum3.tile([P, H], F32, name="pre")
+            pre = psum.tile([P, H], F32, name="pre%d" % m, tag=PRE_BANK[m])
             nc.tensor.matmul_mx(
                 out=pre[:],
                 lhsT=xg[:, m * P : (m + 1) * P].bitcast(FP8X4),
@@ -112,28 +111,33 @@ def tile_moe_dyn_relu2_kernel(
             nc.scalar.activation(
                 pos[:].rearrange("u t p -> u p t"), pre[:].rearrange("u (p t) -> u p t", t=4), ACT.Relu
             )
-            turned = psum3.tile([P, 4, P], F32, name="turned")
+            return pos
+
+        def turn(m, pos):
+            turned = psum.tile([P, 4, P], F32, name="turned%d" % m, tag=TURNED_BANK[m])
             for t in range(4):
                 nc.tensor.transpose(turned[:, t, :], pos[:, t, :], ident[:])
             nc.scalar.activation(
-                hb[m].rearrange("p (u t) -> p u t", t=4),
+                hb[m][:].rearrange("p (u t) -> p u t", t=4),
                 turned[:].rearrange("p t u -> p u t"),
                 ACT.Square,
             )
 
-        def quantise(lo, hi, src, tag):
-            hq = keep.tile([P, (hi - lo) * P], U32, name="hq%d" % lo, tag=tag, align_bytes=64)
-            nc.vector.quantize_mx(out=hq[:].bitcast(FP8X4), scales=hqs[:, lo * P : hi * P], in_=src[:])
-            return hq
-
-        def second_layer(m, hq, cols, apart):
-            acc = psum2.tile([P, 2, P], F32, name="acc")
+        def second_layer(m, tag, apart):
+            hq = keep.tile([P, P], U32, name="hq%d" % m, tag=tag, align_bytes=64)
+            nc.vector.quantize_mx(out=hq[:].bitcast(FP8X4), scales=hqs[:, m * P : (m + 1) * P], in_=hb[m][:])
+            banks = ACC_BANK[m]
+            if banks[0] == banks[1]:
+                acc = psum.tile([P, 2, P], F32, name="acc%d" % m, tag=banks[0])
+                halves = [acc[:, 0, :], acc[:, 1, :]]
+            else:
+                halves = [psum.tile([P, P], F32, name="acc%d_%d" % (m, c), tag=banks[c])[:] for c in range(2)]
             for c in range(2):
                 nc.tensor.matmul_mx(
-                    out=acc[:, c, :],
+                    out=halves[c],
                     lhsT=w2g[m][:, c * P : (c + 1) * P].bitcast(FP8X4),
                     lhsT_scale=w2gs[m][:, c * P : (c + 1) * P],
-                    rhs=hq[:, cols].bitcast(FP8X4),
+                    rhs=hq[:].bitcast(FP8X4),
                     rhs_scale=hqs[:, m * P : (m + 1) * P],
                     start=True,
                     stop=True,
@@ -141,7 +145,7 @@ def tile_moe_dyn_relu2_kernel(
             if apart:
                 for c in range(2):
                     half = keep.tile([P, P], F32, name="y%d_%d" % (m, c), align_bytes=64)
-                    nc.scalar.copy(half[:], acc[:, c, :])
+                    nc.scalar.copy(half[:], halves[c])
                     y[m, c] = half[:]
             else:
                 both = keep.tile([P, 2, P], F32, name="y%d" % m)
@@ -157,50 +161,36 @@ def tile_moe_dyn_relu2_kernel(
         for r in range(4):
             nc.sync.dma_start(out=quadrant_rows(xgs, r), in_=xgs_rows[ROW0 + r : P : 4, :].bitcast(I32))
         nc.sync.dma_start(col2[:], offs3)
-        load_scales(w2s, w2_scales)
+        load_scales(w2s, w2_scales, 0, 1)
         load_words(w2w[:], w2_words)
+        load_scales(w2s, w2_scales, 1, 4)
         nc.sync.dma_start(out=g[:], in_=gate)
         nc.vector.tensor_copy(xg[:], xw[:].bitcast(U32).indirect(tok[:]))
         w1gs = gather_w1("w1gs012", w1s[:], U8, 0, 3) + gather_w1("w1gs34", w1s[:], U8, 3, 5)
         w1g = []
         for m in range(2):
             w1g = w1g + gather_w1("w1g%d" % m, w1_window, U32, m, m + 1)
-            first_layer(m, w1g[m], w1gs[m])
+            turn(m, first_layer(m, w1g[m], w1gs[m]))
         w1g = w1g + gather_w1("w1g23", w1_window, U32, 2, 4)
-        first_layer(2, w1g[2], w1gs[2])
-        first_layer(3, w1g[3], w1gs[3])
+        turn(2, first_layer(2, w1g[2], w1gs[2]))
+        pos3 = first_layer(3, w1g[3], w1gs[3])
         w1gs = w1gs + gather_w1("w1gs5", w1s[:], U8, 5, 6, tag="w1g0")
         w1g = w1g + gather_w1("w1g45", w1_window, U32, 4, 6)
         w2_window = w2w[:].bitcast(U32)
-        w2gs = gather_w2("w2gs", w2s[:], U8, 0, B)
         w2g = gather_w2("w2g01", w2_window, U32, 0, 2)
-        hq = quantise(0, 2, hb01, "hq0")
-        w2g.extend(gather_w2("w2g_rest", w2_window, U32, 2, B, tag="hb01"))
-        first, second = slice(0, P), slice(P, 2 * P)
-        second_layer(0, hq, first, True)
-        second_layer(1, hq, second, False)
-        first_layer(4, w1g[4], w1gs[4])
-        scatter(0, 0)
-        scatter(0, 1)
-        hq = quantise(2, 4, hb23, "y0_0")
-        second_layer(2, hq, first, True)
-        second_layer(3, hq, second, True)
-        hb5 = keep.tile([P, H], BF16, name="hb5", tag="y0_0", align_bytes=64)
-        hb.append(hb5[:])
-        first_layer(5, w1g[5], w1gs[5])
-        scatter(1, 0)
-        scatter(1, 1)
-        scatter(2, 0)
-        scatter(2, 1)
-        hq = quantise(4, 5, hb4, "y2_0")
-        second_layer(4, hq, first, False)
-        scatter(3, 0)
-        scatter(3, 1)
-        hq = quantise(5, 6, hb5, "y3_0")
-        second_layer(5, hq, first, False)
-        scatter(4, 0)
-        scatter(4, 1)
-        scatter(5, 0)
-        nc.sync.dma_start(out=out[:P, :], in_=res[0][:])
-        scatter(5, 1)
+        w2gs = gather_w2("w2gs01", w2s[:], U8, 0, 2)
+        second_layer(0, "hq", True)
+        w2gs.extend(gather_w2("w2gs_rest", w2s[:], U8, 2, B))
+        second_layer(1, "hq", True)
+        w2g.extend(gather_w2("w2g_rest", w2_window, U32, 2, B, tag="hb1"))
+        turn(3, pos3)
+        turn(4, first_layer(4, w1g[4], w1gs[4]))
+        turn(5, first_layer(5, w1g[5], w1gs[5]))
+        for m in range(B):
+            scatter(m, 0)
+            if m == B - 1:
+                nc.sync.dma_start(out=out[:P, :], in_=res[0][:])
+            scatter(m, 1)
+            if m + 2 < B:
+                second_layer(m + 2, "y%d_0" % m, m + 4 < B)
         nc.sync.dma_start(out=out[P:, :], in_=res[1][:])

@@ -20,9 +20,7 @@ P = 128
 S = B * P
 LIST_ROWS = 16
 TOKEN_WINDOW = 1024
-PRE_BANK = "ABABAB"
-TURNED_BANK = "CDEFGD"
-ACC_BANK = ("FG", "HH", "EE", "CC", "AA", "BB")
+PAIRS = B // 2
 ROW0 = P - 16
 
 
@@ -33,7 +31,7 @@ def tile_moe_dyn_relu2_kernel(
     with ExitStack() as ctx:
         lists = ctx.enter_context(tc.tile_pool(name="lists", bufs=1))
         keep = ctx.enter_context(tc.tile_pool(name="keep", bufs=1))
-        ring = ctx.enter_context(tc.tile_pool(name="ring", bufs=2))
+        shared = ctx.enter_context(tc.tile_pool(name="shared", bufs=1))
         psum = ctx.enter_context(tc.psum_pool(name="psum", bufs=1))
 
         def entries(lst, lo, hi):
@@ -59,14 +57,15 @@ def tile_moe_dyn_relu2_kernel(
         xs = keep.tile([P, TOKEN_WINDOW], U8, name="xs")
         w1w = keep.tile([P, E * H], I32, name="w1w")
         w1s = keep.tile([P, E * H], U8, name="w1s")
-        w2s = keep.tile([P, E * N], U8, name="w2s", align_bytes=64)
+        w2s = shared.tile([P, E * N], U8, name="w2s", offset=0, align_bytes=64)
         ident = keep.tile([P, P], F32, name="ident")
         xg = keep.tile([P, S], U32, name="xg", align_bytes=64)
         xgs_rows = keep.tile([P, S], U8, name="xgs_rows")
         xgs = keep.tile([P, S], U8, name="xgs", align_bytes=64)
         hqs = keep.tile([P, S], U8, name="hqs", align_bytes=64)
-        hb = [keep.tile([P, H], BF16, name="hb%d" % m, align_bytes=64) for m in range(B)]
+        hb = [keep.tile([P, 2 * H], BF16, name="hb%d" % j, align_bytes=64) for j in range(PAIRS)]
         y = {}
+        hq = {}
         res = [keep.tile([P, T], F32, name="res%d" % c) for c in range(2)]
 
         nc.vector.memset(w1s[:].bitcast(I32), 0)
@@ -88,75 +87,69 @@ def tile_moe_dyn_relu2_kernel(
             nc.vector.tensor_copy(dst[:], window.indirect(entries(lst, lo * width, hi * width)))
             return [dst[:, j * width : (j + 1) * width] for j in range(hi - lo)]
 
-        def gather_w1(name, window, dtype, lo, hi, tag=None):
-            dst = keep.tile([P, (hi - lo) * H], dtype, name=name, tag=tag or name, align_bytes=64)
+        def gather_w1(name, window, dtype, lo, hi):
+            dst = keep.tile([P, (hi - lo) * H], dtype, name=name, align_bytes=64)
             return gather(dst, window, col1, H, lo, hi)
 
-        def gather_w2(name, window, dtype, lo, hi, tag=None):
-            dst = keep.tile([P, (hi - lo) * N], dtype, name=name, tag=tag or name, align_bytes=64)
+        def gather_w2(name, window, dtype, lo, hi):
+            dst = keep.tile([P, (hi - lo) * N], dtype, name=name, align_bytes=64)
             return gather(dst, window, col2, N, lo, hi)
 
-        def first_layer(m, words, scales):
-            pre = psum.tile([P, H], F32, name="pre%d" % m, tag=PRE_BANK[m])
+        def first_layer(m, tag):
+            pre = psum.tile([P, H], F32, name="pre%d" % m, tag="pre%d" % (m % 2))
             nc.tensor.matmul_mx(
                 out=pre[:],
                 lhsT=xg[:, m * P : (m + 1) * P].bitcast(FP8X4),
                 lhsT_scale=xgs[:, m * P : (m + 1) * P],
-                rhs=words.bitcast(FP8X4),
-                rhs_scale=scales,
+                rhs=w1g[m].bitcast(FP8X4),
+                rhs_scale=w1gs[m],
                 start=True,
                 stop=True,
             )
-            pos = ring.tile([P, 4, P], F32, name="pos")
+            pos = keep.tile([P, 4, P], F32, name="pos%d" % m, tag=tag)
             nc.scalar.activation(
                 pos[:].rearrange("u t p -> u p t"), pre[:].rearrange("u (p t) -> u p t", t=4), ACT.Relu
             )
             return pos
 
         def turn(m, pos):
-            turned = psum.tile([P, 4, P], F32, name="turned%d" % m, tag=TURNED_BANK[m])
+            turned = psum.tile([P, 4, P], F32, name="turned%d" % m, tag="turned%d" % (m % 2))
             for t in range(4):
                 nc.tensor.transpose(turned[:, t, :], pos[:, t, :], ident[:])
             nc.scalar.activation(
-                hb[m][:].rearrange("p (u t) -> p u t", t=4),
+                hb[m // 2][:, (m % 2) * H : (m % 2 + 1) * H].rearrange("p (u t) -> p u t", t=4),
                 turned[:].rearrange("p t u -> p u t"),
                 ACT.Square,
             )
 
-        def second_layer(m, tag, apart):
-            hq = keep.tile([P, P], U32, name="hq%d" % m, tag=tag, align_bytes=64)
-            nc.vector.quantize_mx(out=hq[:].bitcast(FP8X4), scales=hqs[:, m * P : (m + 1) * P], in_=hb[m][:])
-            banks = ACC_BANK[m]
-            if banks[0] == banks[1]:
-                acc = psum.tile([P, 2, P], F32, name="acc%d" % m, tag=banks[0])
-                halves = [acc[:, 0, :], acc[:, 1, :]]
-            else:
-                halves = [psum.tile([P, P], F32, name="acc%d_%d" % (m, c), tag=banks[c])[:] for c in range(2)]
-            for c in range(2):
+        def quantise(j, codes):
+            hq[j] = codes
+            nc.vector.quantize_mx(
+                out=hq[j][:].bitcast(FP8X4), scales=hqs[:, 2 * j * P : 2 * (j + 1) * P], in_=hb[j][:]
+            )
+
+        def second_layer(j, c, tag):
+            acc = psum.tile([P, 2, P], F32, name="acc%d_%d" % (j, c), tag="acc%d_%d" % (j % 2, c))
+            for b in range(2):
+                m = 2 * j + b
                 nc.tensor.matmul_mx(
-                    out=halves[c],
+                    out=acc[:, b, :],
                     lhsT=w2g[m][:, c * P : (c + 1) * P].bitcast(FP8X4),
                     lhsT_scale=w2gs[m][:, c * P : (c + 1) * P],
-                    rhs=hq[:].bitcast(FP8X4),
+                    rhs=hq[j][:, b * P : (b + 1) * P].bitcast(FP8X4),
                     rhs_scale=hqs[:, m * P : (m + 1) * P],
                     start=True,
                     stop=True,
                 )
-            if apart:
-                for c in range(2):
-                    half = keep.tile([P, P], F32, name="y%d_%d" % (m, c), align_bytes=64)
-                    nc.scalar.copy(half[:], halves[c])
-                    y[m, c] = half[:]
-            else:
-                both = keep.tile([P, 2, P], F32, name="y%d" % m)
-                nc.scalar.copy(both[:], acc[:])
-                y[m, 0], y[m, 1] = both[:, 0, :], both[:, 1, :]
+            y[j, c] = keep.tile([P, 2 * P], F32, name="y%d_%d" % (j, c), tag=tag)
+            nc.scalar.copy(y[j, c][:], acc[:].rearrange("p b u -> p (b u)"))
 
-        def scatter(m, c):
-            window = res[c][:].indirect(entries(tok, m * P, (m + 1) * P))
-            nc.vector.tensor_tensor(window, y[m, c], g[:, m * P : (m + 1) * P], MULT)
+        def scatter(j, c):
+            window = res[c][:].indirect(entries(tok, 2 * j * P, 2 * (j + 1) * P))
+            nc.vector.tensor_tensor(window, y[j, c][:], g[:, 2 * j * P : 2 * (j + 1) * P], MULT)
 
         w1_window = w1w[:].bitcast(U32)
+        w2_window = w2w[:].bitcast(U32)
         nc.vector.tensor_copy(xgs_rows[:], xs[:].indirect(tok[:]))
         for r in range(4):
             nc.sync.dma_start(out=quadrant_rows(xgs, r), in_=xgs_rows[ROW0 + r : P : 4, :].bitcast(I32))
@@ -166,31 +159,42 @@ def tile_moe_dyn_relu2_kernel(
         load_scales(w2s, w2_scales, 1, 4)
         nc.sync.dma_start(out=g[:], in_=gate)
         nc.vector.tensor_copy(xg[:], xw[:].bitcast(U32).indirect(tok[:]))
-        w1gs = gather_w1("w1gs012", w1s[:], U8, 0, 3) + gather_w1("w1gs34", w1s[:], U8, 3, 5)
-        w1g = []
-        for m in range(2):
-            w1g = w1g + gather_w1("w1g%d" % m, w1_window, U32, m, m + 1)
-            turn(m, first_layer(m, w1g[m], w1gs[m]))
-        w1g = w1g + gather_w1("w1g23", w1_window, U32, 2, 4)
-        turn(2, first_layer(2, w1g[2], w1gs[2]))
-        pos3 = first_layer(3, w1g[3], w1gs[3])
-        w1gs = w1gs + gather_w1("w1gs5", w1s[:], U8, 5, 6, tag="w1g0")
-        w1g = w1g + gather_w1("w1g45", w1_window, U32, 4, 6)
-        w2_window = w2w[:].bitcast(U32)
+        w1gs = gather_w1("w1gs0123", w1s[:], U8, 0, 4) + gather_w1("w1gs45", w1s[:], U8, 4, 6)
+        w1g = gather_w1("w1g0", w1_window, U32, 0, 1)
+        pos0 = first_layer(0, "posA")
+        w1g.extend(gather_w1("w1g1", w1_window, U32, 1, 2))
+        pos1 = first_layer(1, "posB")
+        turn(0, pos0)
+        turn(1, pos1)
+        w1g.extend(gather_w1("w1g23", w1_window, U32, 2, 4))
+        pos2 = first_layer(2, "posA")
+        pos3 = first_layer(3, "posB")
+        w2gs = gather_w2("w2gs", w2s[:], U8, 0, B)
         w2g = gather_w2("w2g01", w2_window, U32, 0, 2)
-        w2gs = gather_w2("w2gs01", w2s[:], U8, 0, 2)
-        second_layer(0, "hq", True)
-        w2gs.extend(gather_w2("w2gs_rest", w2s[:], U8, 2, B))
-        second_layer(1, "hq", True)
-        w2g.extend(gather_w2("w2g_rest", w2_window, U32, 2, B, tag="hb1"))
+        quantise(0, shared.tile([P, 2 * P], U32, name="hq0", offset=0, align_bytes=64))
+        second_layer(0, 0, "y0_0")
+        rest2 = shared.tile([P, 4 * N], U32, name="w2g_rest", offset=1024, align_bytes=64)
+        w2g.extend(gather(rest2, w2_window, col2, N, 2, B))
+        rest1 = keep.tile([P, 2 * H], U32, name="w1g45", tag="hb0", align_bytes=64)
+        w1g.extend(gather(rest1, w1_window, col1, H, 4, B))
+        turn(2, pos2)
         turn(3, pos3)
-        turn(4, first_layer(4, w1g[4], w1gs[4]))
-        turn(5, first_layer(5, w1g[5], w1gs[5]))
-        for m in range(B):
-            scatter(m, 0)
-            if m == B - 1:
-                nc.sync.dma_start(out=out[:P, :], in_=res[0][:])
-            scatter(m, 1)
-            if m + 2 < B:
-                second_layer(m + 2, "y%d_0" % m, m + 4 < B)
+        second_layer(0, 1, "posB")
+        scatter(0, 0)
+        quantise(1, keep.tile([P, 2 * P], U32, name="hq1", align_bytes=64))
+        scatter(0, 1)
+        pos4 = first_layer(4, "posA")
+        pos5 = first_layer(5, "posC")
+        second_layer(1, 0, "y1_0")
+        turn(4, pos4)
+        turn(5, pos5)
+        second_layer(1, 1, "posC")
+        scatter(1, 0)
+        quantise(2, keep.tile([P, 2 * P], U32, name="hq2", align_bytes=64))
+        scatter(1, 1)
+        second_layer(2, 0, "y2_0")
+        second_layer(2, 1, "y2_1")
+        scatter(2, 0)
+        nc.sync.dma_start(out=out[:P, :], in_=res[0][:])
+        scatter(2, 1)
         nc.sync.dma_start(out=out[P:, :], in_=res[1][:])

@@ -57,13 +57,13 @@ def tile_moe_dyn_relu2_kernel(
         xs = keep.tile([P, TOKEN_WINDOW], U8, name="xs")
         w1w = keep.tile([P, E * H], I32, name="w1w")
         w1s = keep.tile([P, E * H], U8, name="w1s")
-        w2s = shared.tile([P, E * N], U8, name="w2s", offset=0, align_bytes=64)
+        w2s = keep.tile([P, E * N], U8, name="w2s")
         ident = keep.tile([P, P], F32, name="ident")
         xg = keep.tile([P, S], U32, name="xg", align_bytes=64)
         xgs_rows = keep.tile([P, S], U8, name="xgs_rows")
         xgs = keep.tile([P, S], U8, name="xgs", align_bytes=64)
         hqs = keep.tile([P, S], U8, name="hqs", align_bytes=64)
-        hb = [keep.tile([P, 2 * H], BF16, name="hb%d" % j, align_bytes=64) for j in range(PAIRS)]
+        hb = {}
         y = {}
         hq = {}
         res = [keep.tile([P, T], F32, name="res%d" % c) for c in range(2)]
@@ -95,8 +95,8 @@ def tile_moe_dyn_relu2_kernel(
             dst = keep.tile([P, (hi - lo) * N], dtype, name=name, align_bytes=64)
             return gather(dst, window, col2, N, lo, hi)
 
-        def first_layer(m, tag):
-            pre = psum.tile([P, H], F32, name="pre%d" % m, tag="pre%d" % (m % 2))
+        def first_layer(m, bank, pos):
+            pre = psum.tile([P, H], F32, name="pre%d" % m, tag=bank)
             nc.tensor.matmul_mx(
                 out=pre[:],
                 lhsT=xg[:, m * P : (m + 1) * P].bitcast(FP8X4),
@@ -106,14 +106,13 @@ def tile_moe_dyn_relu2_kernel(
                 start=True,
                 stop=True,
             )
-            pos = keep.tile([P, 4, P], F32, name="pos%d" % m, tag=tag)
             nc.scalar.activation(
                 pos[:].rearrange("u t p -> u p t"), pre[:].rearrange("u (p t) -> u p t", t=4), ACT.Relu
             )
             return pos
 
-        def turn(m, pos):
-            turned = psum.tile([P, 4, P], F32, name="turned%d" % m, tag="turned%d" % (m % 2))
+        def turn(m, pos, bank):
+            turned = psum.tile([P, 4, P], F32, name="turned%d" % m, tag=bank)
             for t in range(4):
                 nc.tensor.transpose(turned[:, t, :], pos[:, t, :], ident[:])
             nc.scalar.activation(
@@ -128,8 +127,8 @@ def tile_moe_dyn_relu2_kernel(
                 out=hq[j][:].bitcast(FP8X4), scales=hqs[:, 2 * j * P : 2 * (j + 1) * P], in_=hb[j][:]
             )
 
-        def second_layer(j, c, tag):
-            acc = psum.tile([P, 2, P], F32, name="acc%d_%d" % (j, c), tag="acc%d_%d" % (j % 2, c))
+        def products(j, c, bank):
+            acc = psum.tile([P, 2, P], F32, name="acc%d_%d" % (j, c), tag=bank)
             for b in range(2):
                 m = 2 * j + b
                 nc.tensor.matmul_mx(
@@ -141,12 +140,21 @@ def tile_moe_dyn_relu2_kernel(
                     start=True,
                     stop=True,
                 )
-            y[j, c] = keep.tile([P, 2 * P], F32, name="y%d_%d" % (j, c), tag=tag)
+            return acc
+
+        def leave(j, c, acc, dst):
+            y[j, c] = dst
             nc.scalar.copy(y[j, c][:], acc[:].rearrange("p b u -> p (b u)"))
 
         def scatter(j, c):
             window = res[c][:].indirect(entries(tok, 2 * j * P, 2 * (j + 1) * P))
             nc.vector.tensor_tensor(window, y[j, c][:], g[:, 2 * j * P : 2 * (j + 1) * P], MULT)
+
+        def positive(name):
+            return keep.tile([P, 4, P], F32, name=name, align_bytes=64)
+
+        def results(name):
+            return keep.tile([P, 2 * P], F32, name=name, align_bytes=64)
 
         w1_window = w1w[:].bitcast(U32)
         w2_window = w2w[:].bitcast(U32)
@@ -161,39 +169,41 @@ def tile_moe_dyn_relu2_kernel(
         nc.vector.tensor_copy(xg[:], xw[:].bitcast(U32).indirect(tok[:]))
         w1gs = gather_w1("w1gs0123", w1s[:], U8, 0, 4) + gather_w1("w1gs45", w1s[:], U8, 4, 6)
         w1g = gather_w1("w1g0", w1_window, U32, 0, 1)
-        pos0 = first_layer(0, "posA")
+        pos0 = first_layer(0, "A", positive("pos0"))
         w1g.extend(gather_w1("w1g1", w1_window, U32, 1, 2))
-        pos1 = first_layer(1, "posB")
-        turn(0, pos0)
-        turn(1, pos1)
-        w1g.extend(gather_w1("w1g23", w1_window, U32, 2, 4))
-        pos2 = first_layer(2, "posA")
-        pos3 = first_layer(3, "posB")
-        w2gs = gather_w2("w2gs", w2s[:], U8, 0, B)
-        w2g = gather_w2("w2g01", w2_window, U32, 0, 2)
-        quantise(0, shared.tile([P, 2 * P], U32, name="hq0", offset=0, align_bytes=64))
-        second_layer(0, 0, "y0_0")
-        rest2 = shared.tile([P, 4 * N], U32, name="w2g_rest", offset=1024, align_bytes=64)
-        w2g.extend(gather(rest2, w2_window, col2, N, 2, B))
-        rest1 = keep.tile([P, 2 * H], U32, name="w1g45", tag="hb0", align_bytes=64)
-        w1g.extend(gather(rest1, w1_window, col1, H, 4, B))
-        turn(2, pos2)
-        turn(3, pos3)
-        second_layer(0, 1, "posB")
+        pos1 = first_layer(1, "B", positive("pos1"))
+        hb[0] = keep.tile([P, 2 * H], BF16, name="hb0", align_bytes=64)
+        turn(0, pos0, "C")
+        turn(1, pos1, "D")
+        w1g.extend(gather_w1("w1g2345", w1_window, U32, 2, B))
+        pos2 = first_layer(2, "B", positive("pos2"))
+        pos3 = first_layer(3, "C", shared.tile([P, 4, P], F32, name="pos3", offset=0, align_bytes=64))
+        pos4 = first_layer(4, "D", positive("pos4"))
+        w2g = gather_w2("w2g", w2_window, U32, 0, B)
+        quantise(0, keep.tile([P, 2 * P], U32, name="hq0", align_bytes=64))
+        w2gs = gather_w2("w2gs01", w2s[:], U8, 0, 2)
+        leave(0, 0, products(0, 0, "E"), results("y0_0"))
+        acc = products(0, 1, "F")
+        w2gs.extend(gather_w2("w2gs_rest", w2s[:], U8, 2, B))
+        hb[1] = keep.tile([P, 2 * H], BF16, name="hb1", tag="hq0", align_bytes=64)
+        turn(2, pos2, "A")
+        turn(3, pos3, "E")
+        leave(0, 1, acc, shared.tile([P, 2 * P], F32, name="y0_1", offset=0, align_bytes=64))
         scatter(0, 0)
         quantise(1, keep.tile([P, 2 * P], U32, name="hq1", align_bytes=64))
         scatter(0, 1)
-        pos4 = first_layer(4, "posA")
-        pos5 = first_layer(5, "posC")
-        second_layer(1, 0, "y1_0")
-        turn(4, pos4)
-        turn(5, pos5)
-        second_layer(1, 1, "posC")
+        pos5 = first_layer(5, "A", shared.tile([P, 4, P], F32, name="pos5", offset=1024, align_bytes=64))
+        leave(1, 0, products(1, 0, "G"), results("y1_0"))
+        acc = products(1, 1, "H")
+        hb[2] = keep.tile([P, 2 * H], BF16, name="hb2", tag="hq1", align_bytes=64)
+        turn(4, pos4, "E")
+        turn(5, pos5, "G")
+        leave(1, 1, acc, shared.tile([P, 2 * P], F32, name="y1_1", offset=2048, align_bytes=64))
         scatter(1, 0)
         quantise(2, keep.tile([P, 2 * P], U32, name="hq2", align_bytes=64))
         scatter(1, 1)
-        second_layer(2, 0, "y2_0")
-        second_layer(2, 1, "y2_1")
+        leave(2, 0, products(2, 0, "B"), results("y2_0"))
+        leave(2, 1, products(2, 1, "C"), results("y2_1"))
         scatter(2, 0)
         nc.sync.dma_start(out=out[:P, :], in_=res[0][:])
         scatter(2, 1)

@@ -64,9 +64,8 @@ def tile_moe_dyn_relu2_kernel(
         xgs = keep.tile([P, S], U8, name="xgs", align_bytes=64)
         hqs = keep.tile([P, S], U8, name="hqs", align_bytes=64)
         hb = {}
-        y = {}
         hq = {}
-        res = [keep.tile([P, T], F32, name="res%d" % c) for c in range(2)]
+        res = [keep.tile([P, T], F32, name="res0")]
 
         nc.vector.memset(w1s[:].bitcast(I32), 0)
         nc.vector.memset(xs[:ROW0, :T].bitcast(I32), 0)
@@ -142,13 +141,19 @@ def tile_moe_dyn_relu2_kernel(
                 )
             return acc
 
-        def leave(j, c, acc, dst):
-            y[j, c] = dst
-            nc.scalar.copy(y[j, c][:], acc[:].rearrange("p b u -> p (b u)"))
+        def leave(acc, dst):
+            nc.scalar.copy(dst[:], acc[:].rearrange("p b u -> p (b u)"))
+            return dst
 
-        def scatter(j, c):
-            window = res[c][:].indirect(entries(tok, 2 * j * P, 2 * (j + 1) * P))
-            nc.vector.tensor_tensor(window, y[j, c][:], g[:, 2 * j * P : 2 * (j + 1) * P], MULT)
+        def gates(j):
+            return g[:, 2 * j * P : 2 * (j + 1) * P]
+
+        def gated(j, acc, dst):
+            nc.vector.tensor_tensor(dst[:], acc[:].rearrange("p b u -> p (b u)"), gates(j), MULT)
+            return dst
+
+        def window(c, j):
+            return res[c][:].indirect(entries(tok, 2 * j * P, 2 * (j + 1) * P))
 
         def positive(name):
             return keep.tile([P, 4, P], F32, name=name, align_bytes=64)
@@ -168,43 +173,47 @@ def tile_moe_dyn_relu2_kernel(
         nc.sync.dma_start(out=g[:], in_=gate)
         nc.vector.tensor_copy(xg[:], xw[:].bitcast(U32).indirect(tok[:]))
         w1gs = gather_w1("w1gs0123", w1s[:], U8, 0, 4) + gather_w1("w1gs45", w1s[:], U8, 4, 6)
+        for j in range(PAIRS):
+            hb[j] = keep.tile([P, 2 * H], BF16, name="hb%d" % j, align_bytes=64)
+        codes = [keep.tile([P, 2 * P], U32, name="hq%d" % j, align_bytes=64) for j in range(PAIRS)]
         w1g = gather_w1("w1g0", w1_window, U32, 0, 1)
         pos0 = first_layer(0, "A", positive("pos0"))
         w1g.extend(gather_w1("w1g1", w1_window, U32, 1, 2))
         pos1 = first_layer(1, "B", positive("pos1"))
-        hb[0] = keep.tile([P, 2 * H], BF16, name="hb0", align_bytes=64)
+        w1g.extend(gather_w1("w1g2", w1_window, U32, 2, 3))
         turn(0, pos0, "C")
+        pos2 = first_layer(2, "A", positive("pos2"))
+        w1g.extend(gather_w1("w1g345", w1_window, U32, 3, B))
         turn(1, pos1, "D")
-        w1g.extend(gather_w1("w1g2345", w1_window, U32, 2, B))
-        pos2 = first_layer(2, "B", positive("pos2"))
-        pos3 = first_layer(3, "C", shared.tile([P, 4, P], F32, name="pos3", offset=0, align_bytes=64))
-        pos4 = first_layer(4, "D", positive("pos4"))
+        pos3 = first_layer(3, "B", positive("pos3"))
         w2g = gather_w2("w2g", w2_window, U32, 0, B)
-        quantise(0, keep.tile([P, 2 * P], U32, name="hq0", align_bytes=64))
+        quantise(0, codes[0])
         w2gs = gather_w2("w2gs01", w2s[:], U8, 0, 2)
-        leave(0, 0, products(0, 0, "E"), results("y0_0"))
-        acc = products(0, 1, "F")
         w2gs.extend(gather_w2("w2gs_rest", w2s[:], U8, 2, B))
-        hb[1] = keep.tile([P, 2 * H], BF16, name="hb1", tag="hq0", align_bytes=64)
-        turn(2, pos2, "A")
-        turn(3, pos3, "E")
-        leave(0, 1, acc, shared.tile([P, 2 * P], F32, name="y0_1", offset=0, align_bytes=64))
-        scatter(0, 0)
-        quantise(1, keep.tile([P, 2 * P], U32, name="hq1", align_bytes=64))
-        scatter(0, 1)
-        pos5 = first_layer(5, "A", shared.tile([P, 4, P], F32, name="pos5", offset=1024, align_bytes=64))
-        leave(1, 0, products(1, 0, "G"), results("y1_0"))
-        acc = products(1, 1, "H")
-        hb[2] = keep.tile([P, 2 * H], BF16, name="hb2", tag="hq1", align_bytes=64)
-        turn(4, pos4, "E")
-        turn(5, pos5, "G")
-        leave(1, 1, acc, shared.tile([P, 2 * P], F32, name="y1_1", offset=2048, align_bytes=64))
-        scatter(1, 0)
-        quantise(2, keep.tile([P, 2 * P], U32, name="hq2", align_bytes=64))
-        scatter(1, 1)
-        leave(2, 0, products(2, 0, "B"), results("y2_0"))
-        leave(2, 1, products(2, 1, "C"), results("y2_1"))
-        scatter(2, 0)
+        turn(2, pos2, "E")
+        pos4 = first_layer(4, "C", positive("pos4"))
+        turn(3, pos3, "F")
+        acc00 = products(0, 0, "B")
+        acc01 = products(0, 1, "E")
+        y01 = gated(0, acc01, results("y01"))
+        quantise(1, codes[1])
+        pos5 = first_layer(5, "D", shared.tile([P, 4, P], F32, name="pos5", offset=1024, align_bytes=64))
+        y00 = leave(acc00, results("y00"))
+        nc.vector.tensor_tensor(window(0, 0), y00[:], gates(0), MULT)
+        turn(4, pos4, "G")
+        turn(5, pos5, "H")
+        acc10 = products(1, 0, "A")
+        acc11 = products(1, 1, "C")
+        y11 = gated(1, acc11, results("y11"))
+        quantise(2, codes[2])
+        y10 = leave(acc10, shared.tile([P, 2 * P], F32, name="y10", offset=512, align_bytes=64))
+        res.append(shared.tile([P, T], F32, name="res1", offset=1536, align_bytes=64))
+        nc.scalar.activation(window(1, 0), y01[:], ACT.Copy)
+        nc.vector.tensor_tensor(window(0, 1), y10[:], gates(1), MULT)
+        nc.scalar.activation(window(1, 1), y11[:], ACT.Copy)
+        y21 = gated(2, products(2, 1, "D"), results("y21"))
+        y20 = gated(2, products(2, 0, "F"), results("y20"))
+        nc.scalar.activation(window(1, 2), y21[:], ACT.Copy)
+        nc.scalar.dma_start(out=out[P:, :], in_=res[1][:])
+        nc.vector.tensor_copy(window(0, 2), y20[:])
         nc.sync.dma_start(out=out[:P, :], in_=res[0][:])
-        scatter(2, 1)
-        nc.sync.dma_start(out=out[P:, :], in_=res[1][:])

@@ -173,46 +173,44 @@ def tile_moe_dyn_relu2_kernel(
         nc.sync.dma_start(out=g[:], in_=gate)
         nc.vector.tensor_copy(xg[:], xw[:].bitcast(U32).indirect(tok[:]))
         w1gs = gather_w1("w1gs0123", w1s[:], U8, 0, 4) + gather_w1("w1gs45", w1s[:], U8, 4, 6)
-        for j in range(PAIRS):
-            hb[j] = keep.tile([P, 2 * H], BF16, name="hb%d" % j, align_bytes=64)
-        codes = [keep.tile([P, 2 * P], U32, name="hq%d" % j, align_bytes=64) for j in range(PAIRS)]
-        w1g = gather_w1("w1g0", w1_window, U32, 0, 1)
-        pos0 = first_layer(0, "A", positive("pos0"))
-        w1g.extend(gather_w1("w1g1", w1_window, U32, 1, 2))
-        pos1 = first_layer(1, "B", positive("pos1"))
-        w1g.extend(gather_w1("w1g2", w1_window, U32, 2, 3))
-        turn(0, pos0, "C")
-        pos2 = first_layer(2, "A", positive("pos2"))
-        w1g.extend(gather_w1("w1g345", w1_window, U32, 3, B))
-        turn(1, pos1, "D")
-        pos3 = first_layer(3, "B", positive("pos3"))
+        hb[0] = shared.tile([P, 2 * H], BF16, name="hb0", offset=4096, align_bytes=64)
+        hb[1] = keep.tile([P, 2 * H], BF16, name="hb1", align_bytes=64)
+        hb[2] = keep.tile([P, 2 * H], BF16, name="hb2", align_bytes=64)
+        w1g = []
+        pos = []
+        for m in range(B):
+            w1g.extend(gather_w1("w1g%d" % m, w1_window, U32, m, m + 1))
+            if m < B - 1:
+                pos.append(first_layer(m, "ABCDEF"[m], positive("pos%d" % m)))
+        turn(0, pos[0], "G")
+        turn(1, pos[1], "H")
+        pos.append(first_layer(5, "F", positive("pos5")))
         w2g = gather_w2("w2g", w2_window, U32, 0, B)
-        quantise(0, codes[0])
         w2gs = gather_w2("w2gs01", w2s[:], U8, 0, 2)
-        w2gs.extend(gather_w2("w2gs_rest", w2s[:], U8, 2, B))
-        turn(2, pos2, "E")
-        pos4 = first_layer(4, "C", positive("pos4"))
-        turn(3, pos3, "F")
-        acc00 = products(0, 0, "B")
-        acc01 = products(0, 1, "E")
+        quantise(0, keep.tile([P, 2 * P], U32, name="hq0", align_bytes=64))
+        rest = shared.tile([P, 4 * N], U8, name="w2gs_rest", offset=4096, align_bytes=64)
+        w2gs.extend(gather(rest, w2s[:], col2, N, 2, B))
+        turn(2, pos[2], "A")
+        turn(3, pos[3], "B")
+        acc00 = products(0, 0, "E")
+        acc01 = products(0, 1, "G")
         y01 = gated(0, acc01, results("y01"))
-        quantise(1, codes[1])
-        pos5 = first_layer(5, "D", shared.tile([P, 4, P], F32, name="pos5", offset=1024, align_bytes=64))
+        quantise(1, shared.tile([P, 2 * P], U32, name="hq1", offset=0, align_bytes=64))
         y00 = leave(acc00, results("y00"))
         nc.vector.tensor_tensor(window(0, 0), y00[:], gates(0), MULT)
-        turn(4, pos4, "G")
-        turn(5, pos5, "H")
-        acc10 = products(1, 0, "A")
-        acc11 = products(1, 1, "C")
+        turn(4, pos[4], "C")
+        turn(5, pos[5], "D")
+        acc10 = products(1, 0, "F")
+        acc11 = products(1, 1, "H")
         y11 = gated(1, acc11, results("y11"))
-        quantise(2, codes[2])
-        y10 = leave(acc10, shared.tile([P, 2 * P], F32, name="y10", offset=512, align_bytes=64))
-        res.append(shared.tile([P, T], F32, name="res1", offset=1536, align_bytes=64))
+        quantise(2, keep.tile([P, 2 * P], U32, name="hq2", align_bytes=64))
+        y10 = leave(acc10, results("y10"))
+        res.append(shared.tile([P, T], F32, name="res1", offset=0, align_bytes=64))
         nc.scalar.activation(window(1, 0), y01[:], ACT.Copy)
         nc.vector.tensor_tensor(window(0, 1), y10[:], gates(1), MULT)
+        y20 = gated(2, products(2, 0, "A"), results("y20"))
+        y21 = gated(2, products(2, 1, "B"), results("y21"))
         nc.scalar.activation(window(1, 1), y11[:], ACT.Copy)
-        y21 = gated(2, products(2, 1, "D"), results("y21"))
-        y20 = gated(2, products(2, 0, "F"), results("y20"))
         nc.scalar.activation(window(1, 2), y21[:], ACT.Copy)
         nc.scalar.dma_start(out=out[P:, :], in_=res[1][:])
         nc.vector.tensor_copy(window(0, 2), y20[:])

@@ -19,8 +19,7 @@ MULT = mybir.AluOpType.mult
 P = 128
 S = B * P
 LIST_ROWS = 16
-TOKEN_WINDOW = 1024
-PAIRS = B // 2
+EARLY = 4
 ROW0 = P - 16
 
 
@@ -43,85 +42,105 @@ def tile_moe_dyn_relu2_kernel(
         def quadrant_rows(plane, r):
             return plane[r:P:32, :].bitcast(I32)
 
-        def load_scales(plane, src, lo=0, hi=4):
+        def load_scales(plane, src):
             rows = src[0].rearrange("(q r) n -> r q n", r=4)
-            for r in range(lo, hi):
+            for r in range(4):
                 nc.sync.dma_start(out=quadrant_rows(plane, r), in_=rows[r].bitcast(I32))
+
+        def move_scales(plane, rows):
+            for r in range(4):
+                nc.sync.dma_start(out=quadrant_rows(plane, r), in_=rows[ROW0 + r : P : 4, :].bitcast(I32))
+
+        def placed(name, shape, dtype, offset):
+            return shared.tile(shape, dtype, name=name, offset=offset, align_bytes=64)
+
+        def kept(name, shape, dtype):
+            return keep.tile(shape, dtype, name=name, align_bytes=64)
 
         tok = lists.tile([P, S // LIST_ROWS], U16, name="tok")
         col1 = lists.tile([P, B * H // LIST_ROWS], U16, name="col1")
         col2 = lists.tile([P, B * N // LIST_ROWS], U16, name="col2")
-        xw = keep.tile([P, TOKEN_WINDOW], I32, name="xw")
-        w2w = keep.tile([P, E * N], I32, name="w2w")
-        g = keep.tile([P, S], F32, name="g")
-        xs = keep.tile([P, TOKEN_WINDOW], U8, name="xs")
-        w1w = keep.tile([P, E * H], I32, name="w1w")
-        w1s = keep.tile([P, E * H], U8, name="w1s")
-        w2s = keep.tile([P, E * N], U8, name="w2s")
-        ident = keep.tile([P, P], F32, name="ident")
-        xg = keep.tile([P, S], U32, name="xg", align_bytes=64)
-        xgs_rows = keep.tile([P, S], U8, name="xgs_rows")
-        xgs = keep.tile([P, S], U8, name="xgs", align_bytes=64)
-        hqs = keep.tile([P, S], U8, name="hqs", align_bytes=64)
-        hb = {}
-        hq = {}
-        res = [keep.tile([P, T], F32, name="res0")]
+        W1S_AT, XW_AT, W1G0_AT, HQ0_AT, POS2_AT = 0, 10240, 14336, 16384, 21504
+        w1s = placed("w1s", [P, E * H], U8, W1S_AT)
+        xs = kept("xs", [P, T], U8)
+        xw = placed("xw", [P, T], I32, XW_AT)
+        w1w = kept("w1w", [P, E * H], I32)
+        w1p = kept("w1p", [P, B * H], U8)
+        ident = kept("ident", [P, P], F32)
+        hqs = kept("hqs", [P, S], U8)
 
-        nc.vector.memset(w1s[:].bitcast(I32), 0)
-        nc.vector.memset(xs[:ROW0, :T].bitcast(I32), 0)
-        nc.vector.memset(xs[:, T:].bitcast(I32), 0)
-        nc.vector.memset(xw[:, T:], 0)
-        nc.vector.memset(w2s[:].bitcast(I32), 0)
-        nc.vector.memset(xgs[:].bitcast(I32), 0)
+        nc.vector.memset(w1s[:ROW0, :].bitcast(I32), 0)
+        nc.vector.memset(xs[:].bitcast(I32), 0)
+        nc.vector.memset(w1p[:].bitcast(I32), 0)
         make_identity(nc, ident[:])
 
-        nc.sync.dma_start(tok[:], offs)
-        nc.sync.dma_start(out=xs[ROW0:, :T].bitcast(I32), in_=x_scales[0].bitcast(I32))
         nc.sync.dma_start(col1[:], offs2)
-        load_words(xw[:, :T], x_words)
-        load_scales(w1s, w1_scales)
+        nc.sync.dma_start(out=w1s[ROW0:, :].bitcast(I32), in_=w1_scales[0].bitcast(I32))
+        nc.sync.dma_start(tok[:], offs)
+        load_scales(xs, x_scales)
+        load_words(xw[:], x_words)
         load_words(w1w[:], w1_words)
+        nc.sync.dma_start(col2[:], offs3)
 
         def gather(dst, window, lst, width, lo, hi):
-            nc.vector.tensor_copy(dst[:], window.indirect(entries(lst, lo * width, hi * width)))
+            nc.vector.tensor_copy(dst[:, :], window.indirect(entries(lst, lo * width, hi * width)))
             return [dst[:, j * width : (j + 1) * width] for j in range(hi - lo)]
 
-        def gather_w1(name, window, dtype, lo, hi):
-            dst = keep.tile([P, (hi - lo) * H], dtype, name=name, align_bytes=64)
-            return gather(dst, window, col1, H, lo, hi)
+        rows = kept("rows", [P, B * H], U8)
+        gather(rows[:, : 3 * H], w1s[:], col1, H, 0, 3)
+        gather(rows[:, 3 * H :], w1s[:], col1, H, 3, B)
+        move_scales(w1p, rows)
+        w2w = placed("w2w", [P, E * N], I32, W1S_AT + E * N)
+        load_words(w2w[:], w2_words)
+        w2s = placed("w2s", [P, E * N], U8, W1S_AT)
+        nc.gpsimd.memset(w2s[:].bitcast(I32), 0)
+        load_scales(w2s, w2_scales)
+        xgs = gather(kept("xgs_early", [P, EARLY * P], U8), xs[:], tok, P, 0, EARLY)
+        w1gs = [w1p[:, m * H : (m + 1) * H] for m in range(B)]
+        x_window = xw[:].bitcast(U32)
+        w1_window = w1w[:].bitcast(U32)
+        w2_window = w2w[:].bitcast(U32)
+        xg = gather(kept("xg_early", [P, EARLY * P], U32), x_window, tok, P, 0, EARLY)
 
-        def gather_w2(name, window, dtype, lo, hi):
-            dst = keep.tile([P, (hi - lo) * N], dtype, name=name, align_bytes=64)
-            return gather(dst, window, col2, N, lo, hi)
+        w1g = {}
+        pos = {}
+        turned = {}
+        hq = [placed("hq0", [P, 2 * P], U32, HQ0_AT)] + [kept("hq%d" % j, [P, 2 * P], U32) for j in (1, 2)]
+        hb = [kept("hb%d" % j, [P, 2 * H], BF16) for j in (0, 1)] + [placed("hb2", [P, 2 * H], BF16, HQ0_AT)]
+        res = [kept("res%d" % c, [P, T], F32) for c in range(2)]
 
-        def first_layer(m, bank, pos):
+        def gather_w1(m, dst):
+            w1g[m] = gather(dst, w1_window, col1, H, m, m + 1)[0]
+
+        def first_layer(m, bank):
             pre = psum.tile([P, H], F32, name="pre%d" % m, tag=bank)
             nc.tensor.matmul_mx(
                 out=pre[:],
-                lhsT=xg[:, m * P : (m + 1) * P].bitcast(FP8X4),
-                lhsT_scale=xgs[:, m * P : (m + 1) * P],
+                lhsT=xg[m].bitcast(FP8X4),
+                lhsT_scale=xgs[m],
                 rhs=w1g[m].bitcast(FP8X4),
                 rhs_scale=w1gs[m],
                 start=True,
                 stop=True,
             )
+            pos[m] = placed("pos2", [P, 4, P], F32, POS2_AT) if m == 2 else kept("pos%d" % m, [P, 4, P], F32)
             nc.scalar.activation(
-                pos[:].rearrange("u t p -> u p t"), pre[:].rearrange("u (p t) -> u p t", t=4), ACT.Relu
+                pos[m][:].rearrange("u t p -> u p t"), pre[:].rearrange("u (p t) -> u p t", t=4), ACT.Relu
             )
-            return pos
 
-        def turn(m, pos, bank):
-            turned = psum.tile([P, 4, P], F32, name="turned%d" % m, tag=bank)
+        def turn(m, bank):
+            turned[m] = psum.tile([P, 4, P], F32, name="turned%d" % m, tag=bank)
             for t in range(4):
-                nc.tensor.transpose(turned[:, t, :], pos[:, t, :], ident[:])
+                nc.tensor.transpose(turned[m][:, t, :], pos[m][:, t, :], ident[:])
+
+        def square(m):
             nc.scalar.activation(
                 hb[m // 2][:, (m % 2) * H : (m % 2 + 1) * H].rearrange("p (u t) -> p u t", t=4),
-                turned[:].rearrange("p t u -> p u t"),
+                turned[m][:].rearrange("p t u -> p u t"),
                 ACT.Square,
             )
 
-        def quantise(j, codes):
-            hq[j] = codes
+        def quantise(j):
             nc.vector.quantize_mx(
                 out=hq[j][:].bitcast(FP8X4), scales=hqs[:, 2 * j * P : 2 * (j + 1) * P], in_=hb[j][:]
             )
@@ -139,77 +158,71 @@ def tile_moe_dyn_relu2_kernel(
                     start=True,
                     stop=True,
                 )
-            return acc
+            return acc[:].rearrange("p b u -> p (b u)")
 
-        def leave(acc, dst):
-            nc.scalar.copy(dst[:], acc[:].rearrange("p b u -> p (b u)"))
+        def leave(name, acc):
+            dst = kept(name, [P, 2 * P], F32)
+            nc.scalar.copy(dst[:], acc)
             return dst
 
         def gates(j):
             return g[:, 2 * j * P : 2 * (j + 1) * P]
 
-        def gated(j, acc, dst):
-            nc.vector.tensor_tensor(dst[:], acc[:].rearrange("p b u -> p (b u)"), gates(j), MULT)
+        def gated(name, j, acc):
+            dst = kept(name, [P, 2 * P], F32)
+            nc.vector.tensor_tensor(dst[:], acc, gates(j), MULT)
             return dst
 
         def window(c, j):
             return res[c][:].indirect(entries(tok, 2 * j * P, 2 * (j + 1) * P))
 
-        def positive(name):
-            return keep.tile([P, 4, P], F32, name=name, align_bytes=64)
-
-        def results(name):
-            return keep.tile([P, 2 * P], F32, name=name, align_bytes=64)
-
-        w1_window = w1w[:].bitcast(U32)
-        w2_window = w2w[:].bitcast(U32)
-        nc.vector.tensor_copy(xgs_rows[:], xs[:].indirect(tok[:]))
-        for r in range(4):
-            nc.sync.dma_start(out=quadrant_rows(xgs, r), in_=xgs_rows[ROW0 + r : P : 4, :].bitcast(I32))
-        nc.sync.dma_start(col2[:], offs3)
-        load_scales(w2s, w2_scales, 0, 1)
-        load_words(w2w[:], w2_words)
-        load_scales(w2s, w2_scales, 1, 4)
+        gather_w1(0, placed("w1g0", [P, H], U32, W1G0_AT))
+        first_layer(0, "A")
+        for m in (1, 2):
+            gather_w1(m, kept("w1g%d" % m, [P, H], U32))
+            first_layer(m, "ABC"[m])
+        turn(0, "D")
+        turn(1, "E")
+        square(0)
+        square(1)
+        gather_w1(3, kept("w1g3", [P, H], U32))
+        first_layer(3, "B")
+        for m in (4, 5):
+            gather_w1(m, kept("w1g%d" % m, [P, H], U32))
+        xgs.extend(gather(placed("xgs_late", [P, 2 * P], U8, W1G0_AT), xs[:], tok, P, EARLY, B))
+        xg.extend(gather(placed("xg_late", [P, 2 * P], U32, W1G0_AT + 256), x_window, tok, P, EARLY, B))
+        turn(2, "D")
+        g = placed("g", [P, S], F32, POS2_AT - 2560)
         nc.sync.dma_start(out=g[:], in_=gate)
-        nc.vector.tensor_copy(xg[:], xw[:].bitcast(U32).indirect(tok[:]))
-        w1gs = gather_w1("w1gs0123", w1s[:], U8, 0, 4) + gather_w1("w1gs45", w1s[:], U8, 4, 6)
-        hb[0] = shared.tile([P, 2 * H], BF16, name="hb0", offset=4096, align_bytes=64)
-        hb[1] = keep.tile([P, 2 * H], BF16, name="hb1", align_bytes=64)
-        hb[2] = keep.tile([P, 2 * H], BF16, name="hb2", align_bytes=64)
-        w1g = []
-        pos = []
-        for m in range(B):
-            w1g.extend(gather_w1("w1g%d" % m, w1_window, U32, m, m + 1))
-            if m < B - 1:
-                pos.append(first_layer(m, "ABCDEF"[m], positive("pos%d" % m)))
-        turn(0, pos[0], "G")
-        turn(1, pos[1], "H")
-        pos.append(first_layer(5, "F", positive("pos5")))
-        w2g = gather_w2("w2g", w2_window, U32, 0, B)
-        w2gs = gather_w2("w2gs01", w2s[:], U8, 0, 2)
-        quantise(0, keep.tile([P, 2 * P], U32, name="hq0", align_bytes=64))
-        rest = shared.tile([P, 4 * N], U8, name="w2gs_rest", offset=4096, align_bytes=64)
-        w2gs.extend(gather(rest, w2s[:], col2, N, 2, B))
-        turn(2, pos[2], "A")
-        turn(3, pos[3], "B")
-        acc00 = products(0, 0, "E")
+        first_layer(4, "E")
+        square(2)
+        w2g = gather(kept("w2g_first", [P, 2 * N], U32), w2_window, col2, N, 0, 2)
+        w2gs = gather(kept("w2gs_first", [P, 2 * N], U8), w2s[:], col2, N, 0, 2)
+        quantise(0)
+        w2gs.extend(gather(placed("w2gs_rest", [P, 4 * N], U8, POS2_AT + 512), w2s[:], col2, N, 2, B))
+        w2g.extend(gather(placed("w2g_rest", [P, 4 * N], U32, POS2_AT + 1536), w2_window, col2, N, 2, B))
+        first_layer(5, "B")
+        turn(3, "A")
+        square(3)
+        acc00 = products(0, 0, "F")
         acc01 = products(0, 1, "G")
-        y01 = gated(0, acc01, results("y01"))
-        quantise(1, shared.tile([P, 2 * P], U32, name="hq1", offset=0, align_bytes=64))
-        y00 = leave(acc00, results("y00"))
+        quantise(1)
+        y01 = gated("y01", 0, acc01)
+        y00 = leave("y00", acc00)
         nc.vector.tensor_tensor(window(0, 0), y00[:], gates(0), MULT)
-        turn(4, pos[4], "C")
-        turn(5, pos[5], "D")
-        acc10 = products(1, 0, "F")
-        acc11 = products(1, 1, "H")
-        y11 = gated(1, acc11, results("y11"))
-        quantise(2, keep.tile([P, 2 * P], U32, name="hq2", align_bytes=64))
-        y10 = leave(acc10, results("y10"))
-        res.append(shared.tile([P, T], F32, name="res1", offset=0, align_bytes=64))
+        turn(4, "H")
+        turn(5, "C")
+        square(4)
+        square(5)
+        acc10 = products(1, 0, "B")
+        acc11 = products(1, 1, "D")
+        y11 = gated("y11", 1, acc11)
+        quantise(2)
+        y10 = leave("y10", acc10)
         nc.scalar.activation(window(1, 0), y01[:], ACT.Copy)
         nc.vector.tensor_tensor(window(0, 1), y10[:], gates(1), MULT)
-        y20 = gated(2, products(2, 0, "A"), results("y20"))
-        y21 = gated(2, products(2, 1, "B"), results("y21"))
+        y20 = gated("y20", 2, products(2, 0, "A"))
+        y21 = gated("y21", 2, products(2, 1, "E"))
         nc.scalar.activation(window(1, 1), y11[:], ACT.Copy)
         nc.scalar.activation(window(1, 2), y21[:], ACT.Copy)
         nc.scalar.dma_start(out=out[P:, :], in_=res[1][:])

@@ -19,7 +19,7 @@ MULT = mybir.AluOpType.mult
 P = 128
 S = B * P
 LIST_ROWS = 16
-EARLY = 4
+SCALE_WINDOW = 1024
 ROW0 = P - 16
 
 
@@ -60,57 +60,58 @@ def tile_moe_dyn_relu2_kernel(
         tok = lists.tile([P, S // LIST_ROWS], U16, name="tok")
         col1 = lists.tile([P, B * H // LIST_ROWS], U16, name="col1")
         col2 = lists.tile([P, B * N // LIST_ROWS], U16, name="col2")
-        W1S_AT, XW_AT, W1G0_AT, HQ0_AT, POS2_AT = 0, 10240, 14336, 16384, 21504
-        w1s = placed("w1s", [P, E * H], U8, W1S_AT)
-        xs = kept("xs", [P, T], U8)
-        xw = placed("xw", [P, T], I32, XW_AT)
+        ROWS_AT, HQ0_AT = 1536, 8192
+        w1s = kept("w1s", [P, E * H], U8)
+        w2s = kept("w2s", [P, E * N], U8)
+        g = kept("g", [P, S], F32)
+        w2w = kept("w2w", [P, E * N], I32)
+        xs = kept("xs", [P, SCALE_WINDOW], U8)
+        xw = kept("xw", [P, T], I32)
         w1w = kept("w1w", [P, E * H], I32)
         w1p = kept("w1p", [P, B * H], U8)
         ident = kept("ident", [P, P], F32)
         hqs = kept("hqs", [P, S], U8)
 
-        nc.vector.memset(w1s[:ROW0, :].bitcast(I32), 0)
         nc.vector.memset(xs[:].bitcast(I32), 0)
+        nc.vector.memset(w1s[:ROW0, :].bitcast(I32), 0)
         nc.vector.memset(w1p[:].bitcast(I32), 0)
+        nc.vector.memset(w2s[:].bitcast(I32), 0)
         make_identity(nc, ident[:])
 
         nc.sync.dma_start(col1[:], offs2)
         nc.sync.dma_start(out=w1s[ROW0:, :].bitcast(I32), in_=w1_scales[0].bitcast(I32))
         nc.sync.dma_start(tok[:], offs)
-        load_scales(xs, x_scales)
-        load_words(xw[:], x_words)
+        load_scales(xs[:, :T], x_scales)
         load_words(w1w[:], w1_words)
-        nc.sync.dma_start(col2[:], offs3)
+        load_words(xw[:], x_words)
 
         def gather(dst, window, lst, width, lo, hi):
             nc.vector.tensor_copy(dst[:, :], window.indirect(entries(lst, lo * width, hi * width)))
             return [dst[:, j * width : (j + 1) * width] for j in range(hi - lo)]
 
-        rows = kept("rows", [P, B * H], U8)
+        rows = placed("rows", [P, B * H], U8, ROWS_AT)
         gather(rows[:, : 3 * H], w1s[:], col1, H, 0, 3)
         gather(rows[:, 3 * H :], w1s[:], col1, H, 3, B)
         move_scales(w1p, rows)
-        w2w = placed("w2w", [P, E * N], I32, W1S_AT + E * N)
+        nc.sync.dma_start(col2[:], offs3)
         load_words(w2w[:], w2_words)
-        w2s = placed("w2s", [P, E * N], U8, W1S_AT)
-        nc.gpsimd.memset(w2s[:].bitcast(I32), 0)
         load_scales(w2s, w2_scales)
-        xgs = gather(kept("xgs_early", [P, EARLY * P], U8), xs[:], tok, P, 0, EARLY)
+        nc.sync.dma_start(out=g[:], in_=gate)
+        xgs = gather(kept("xgs", [P, S], U8), xs[:], tok, P, 0, B)
         w1gs = [w1p[:, m * H : (m + 1) * H] for m in range(B)]
         x_window = xw[:].bitcast(U32)
         w1_window = w1w[:].bitcast(U32)
         w2_window = w2w[:].bitcast(U32)
-        xg = gather(kept("xg_early", [P, EARLY * P], U32), x_window, tok, P, 0, EARLY)
 
-        w1g = {}
+        w1g = []
         pos = {}
         turned = {}
         hq = [placed("hq0", [P, 2 * P], U32, HQ0_AT)] + [kept("hq%d" % j, [P, 2 * P], U32) for j in (1, 2)]
         hb = [kept("hb%d" % j, [P, 2 * H], BF16) for j in (0, 1)] + [placed("hb2", [P, 2 * H], BF16, HQ0_AT)]
         res = [kept("res%d" % c, [P, T], F32) for c in range(2)]
 
-        def gather_w1(m, dst):
-            w1g[m] = gather(dst, w1_window, col1, H, m, m + 1)[0]
+        def gather_w1(lo, hi, dst):
+            w1g.extend(gather(dst, w1_window, col1, H, lo, hi))
 
         def first_layer(m, bank):
             pre = psum.tile([P, H], F32, name="pre%d" % m, tag=bank)
@@ -123,7 +124,7 @@ def tile_moe_dyn_relu2_kernel(
                 start=True,
                 stop=True,
             )
-            pos[m] = placed("pos2", [P, 4, P], F32, POS2_AT) if m == 2 else kept("pos%d" % m, [P, 4, P], F32)
+            pos[m] = kept("pos%d" % m, [P, 4, P], F32)
             nc.scalar.activation(
                 pos[m][:].rearrange("u t p -> u p t"), pre[:].rearrange("u (p t) -> u p t", t=4), ACT.Relu
             )
@@ -176,38 +177,34 @@ def tile_moe_dyn_relu2_kernel(
         def window(c, j):
             return res[c][:].indirect(entries(tok, 2 * j * P, 2 * (j + 1) * P))
 
-        gather_w1(0, placed("w1g0", [P, H], U32, W1G0_AT))
-        first_layer(0, "A")
-        for m in (1, 2):
-            gather_w1(m, kept("w1g%d" % m, [P, H], U32))
+        for m in (0, 1):
+            gather_w1(m, m + 1, kept("w1g%d" % m, [P, H], U32))
+        xg = gather(kept("xg_first", [P, 2 * P], U32), x_window, tok, P, 0, 2)
+        xg.extend(gather(kept("xg_rest", [P, 4 * P], U32), x_window, tok, P, 2, B))
+        gather_w1(2, 3, placed("w1g2", [P, H], U32, ROWS_AT - 1536))
+        gather_w1(3, 4, placed("w1g3", [P, H], U32, ROWS_AT + 512))
+        gather_w1(4, 6, placed("w1g45", [P, 2 * H], U32, ROWS_AT + 2560))
+        for m in range(3):
             first_layer(m, "ABC"[m])
         turn(0, "D")
         turn(1, "E")
         square(0)
         square(1)
-        gather_w1(3, kept("w1g3", [P, H], U32))
         first_layer(3, "B")
-        for m in (4, 5):
-            gather_w1(m, kept("w1g%d" % m, [P, H], U32))
-        xgs.extend(gather(placed("xgs_late", [P, 2 * P], U8, W1G0_AT), xs[:], tok, P, EARLY, B))
-        xg.extend(gather(placed("xg_late", [P, 2 * P], U32, W1G0_AT + 256), x_window, tok, P, EARLY, B))
         turn(2, "D")
-        g = placed("g", [P, S], F32, POS2_AT - 2560)
-        nc.sync.dma_start(out=g[:], in_=gate)
         first_layer(4, "E")
         square(2)
-        w2g = gather(kept("w2g_first", [P, 2 * N], U32), w2_window, col2, N, 0, 2)
-        w2gs = gather(kept("w2gs_first", [P, 2 * N], U8), w2s[:], col2, N, 0, 2)
+        w2g = gather(kept("w2g", [P, B * N], U32), w2_window, col2, N, 0, B)
         quantise(0)
-        w2gs.extend(gather(placed("w2gs_rest", [P, 4 * N], U8, POS2_AT + 512), w2s[:], col2, N, 2, B))
-        w2g.extend(gather(placed("w2g_rest", [P, 4 * N], U32, POS2_AT + 1536), w2_window, col2, N, 2, B))
+        w2gs = gather(kept("w2gs_first", [P, 2 * N], U8), w2s[:], col2, N, 0, 2)
+        w2gs.extend(gather(kept("w2gs_rest", [P, 4 * N], U8), w2s[:], col2, N, 2, B))
         first_layer(5, "B")
         turn(3, "A")
         square(3)
         acc00 = products(0, 0, "F")
         acc01 = products(0, 1, "G")
-        quantise(1)
         y01 = gated("y01", 0, acc01)
+        quantise(1)
         y00 = leave("y00", acc00)
         nc.vector.tensor_tensor(window(0, 0), y00[:], gates(0), MULT)
         turn(4, "H")

@@ -126,7 +126,7 @@ def tile_moe_dyn_relu2_kernel(
             )
             pos[m] = kept("pos%d" % m, [P, 4, P], F32)
             nc.scalar.activation(
-                pos[m][:].rearrange("u t p -> u p t"), pre[:].rearrange("u (p t) -> u p t", t=4), ACT.Relu
+                pos[m][:], pre[:].rearrange("u (p t) -> u t p", t=4), ACT.Relu
             )
 
         def turn(m, bank):

@@ -222,6 +222,6 @@ def tile_moe_dyn_relu2_kernel(
         y21 = gated("y21", 2, products(2, 1, "E"))
         nc.scalar.activation(window(1, 1), y11[:], ACT.Copy)
         nc.scalar.activation(window(1, 2), y21[:], ACT.Copy)
-        nc.scalar.dma_start(out=out[P:, :], in_=res[1][:])
+        nc.sync.dma_start(out=out[P:, :], in_=res[1][:])
         nc.vector.tensor_copy(window(0, 2), y20[:])
         nc.sync.dma_start(out=out[:P, :], in_=res[0][:])

from contextlib import ExitStack

import concourse.mybir as mybir
from concourse.masks import make_identity

K, T, E, B, H, N = 512, 768, 8, 6, 512, 256
FLOPS = 2 * B * 128 * (K * H + H * N)

F32 = mybir.dt.float32
BF16 = mybir.dt.bfloat16
I32 = mybir.dt.int32
U32 = mybir.dt.uint32
U16 = mybir.dt.uint16
U8 = mybir.dt.uint8
FP8X4 = mybir.dt.float8_e4m3fn_x4
ACT = mybir.ActivationFunctionType
MULT = mybir.AluOpType.mult

P = 128
S = B * P
LIST_ROWS = 16
SCALE_WINDOW = 1024
ROW0 = P - 16


def tile_moe_dyn_relu2_kernel(
    tc, x_words, x_scales, w1_words, w1_scales, w2_words, w2_scales, gate, offs, offs2, offs3, out
):
    nc = tc.nc
    with ExitStack() as ctx:
        lists = ctx.enter_context(tc.tile_pool(name="lists", bufs=1))
        keep = ctx.enter_context(tc.tile_pool(name="keep", bufs=1))
        shared = ctx.enter_context(tc.tile_pool(name="shared", bufs=1))
        psum = ctx.enter_context(tc.psum_pool(name="psum", bufs=1))

        def entries(lst, lo, hi):
            return lst[:, lo // LIST_ROWS : hi // LIST_ROWS]

        def load_words(dst, src):
            nc.sync.dma_start(out=dst, in_=src[0].rearrange("p n t -> p (n t)").bitcast(I32))

        def quadrant_rows(plane, r):
            return plane[r:P:32, :].bitcast(I32)

        def load_scales(plane, src):
            rows = src[0].rearrange("(q r) n -> r q n", r=4)
            for r in range(4):
                nc.sync.dma_start(out=quadrant_rows(plane, r), in_=rows[r].bitcast(I32))

        def move_scales(plane, rows):
            for r in range(4):
                nc.sync.dma_start(out=quadrant_rows(plane, r), in_=rows[ROW0 + r : P : 4, :].bitcast(I32))

        def placed(name, shape, dtype, offset):
            return shared.tile(shape, dtype, name=name, offset=offset, align_bytes=64)

        def kept(name, shape, dtype):
            return keep.tile(shape, dtype, name=name, align_bytes=64)

        tok = lists.tile([P, S // LIST_ROWS], U16, name="tok")
        col1 = lists.tile([P, B * H // LIST_ROWS], U16, name="col1")
        col2 = lists.tile([P, B * N // LIST_ROWS], U16, name="col2")
        ROWS_AT, HQ0_AT = 1536, 8192
        w1s = kept("w1s", [P, E * H], U8)
        w2s = kept("w2s", [P, E * N], U8)
        g = kept("g", [P, S], F32)
        w2w = kept("w2w", [P, E * N], I32)
        xs = kept("xs", [P, SCALE_WINDOW], U8)
        xw = kept("xw", [P, T], I32)
        w1w = kept("w1w", [P, E * H], I32)
        w1p = kept("w1p", [P, B * H], U8)
        ident = kept("ident", [P, P], F32)
        hqs = kept("hqs", [P, S], U8)

        nc.vector.memset(xs[:].bitcast(I32), 0)
        nc.vector.memset(w1s[:ROW0, :].bitcast(I32), 0)
        nc.vector.memset(w1p[:].bitcast(I32), 0)
        nc.vector.memset(w2s[:].bitcast(I32), 0)
        make_identity(nc, ident[:])

        nc.sync.dma_start(col1[:], offs2)
        nc.sync.dma_start(out=w1s[ROW0:, :].bitcast(I32), in_=w1_scales[0].bitcast(I32))
        nc.sync.dma_start(tok[:], offs)
        load_scales(xs[:, :T], x_scales)
        load_words(w1w[:], w1_words)
        load_words(xw[:], x_words)

        def gather(dst, window, lst, width, lo, hi):
            nc.vector.tensor_copy(dst[:, :], window.indirect(entries(lst, lo * width, hi * width)))
            return [dst[:, j * width : (j + 1) * width] for j in range(hi - lo)]

        rows = placed("rows", [P, B * H], U8, ROWS_AT)
        gather(rows[:, : 3 * H], w1s[:], col1, H, 0, 3)
        gather(rows[:, 3 * H :], w1s[:], col1, H, 3, B)
        move_scales(w1p, rows)
        nc.sync.dma_start(col2[:], offs3)
        load_words(w2w[:], w2_words)
        load_scales(w2s, w2_scales)
        nc.sync.dma_start(out=g[:], in_=gate)
        xgs = gather(kept("xgs", [P, S], U8), xs[:], tok, P, 0, B)
        w1gs = [w1p[:, m * H : (m + 1) * H] for m in range(B)]
        x_window = xw[:].bitcast(U32)
        w1_window = w1w[:].bitcast(U32)
        w2_window = w2w[:].bitcast(U32)

        w1g = []
        pos = {}
        turned = {}
        hq = [placed("hq0", [P, 2 * P], U32, HQ0_AT)] + [kept("hq%d" % j, [P, 2 * P], U32) for j in (1, 2)]
        hb = [kept("hb%d" % j, [P, 2 * H], BF16) for j in (0, 1)] + [placed("hb2", [P, 2 * H], BF16, HQ0_AT)]
        res = [kept("res%d" % c, [P, T], F32) for c in range(2)]

        def gather_w1(lo, hi, dst):
            w1g.extend(gather(dst, w1_window, col1, H, lo, hi))

        def first_layer(m, bank):
            pre = psum.tile([P, H], F32, name="pre%d" % m, tag=bank)
            nc.tensor.matmul_mx(
                out=pre[:],
                lhsT=xg[m].bitcast(FP8X4),
                lhsT_scale=xgs[m],
                rhs=w1g[m].bitcast(FP8X4),
                rhs_scale=w1gs[m],
                start=True,
                stop=True,
            )
            pos[m] = kept("pos%d" % m, [P, 4, P], F32)
            nc.scalar.activation(
                pos[m][:], pre[:].rearrange("u (p t) -> u t p", t=4), ACT.Relu
            )

        def turn(m, bank):
            turned[m] = psum.tile([P, 4, P], F32, name="turned%d" % m, tag=bank)
            for t in range(4):
                nc.tensor.transpose(turned[m][:, t, :], pos[m][:, t, :], ident[:])

        def square(m):
            nc.scalar.activation(
                hb[m // 2][:, (m % 2) * H : (m % 2 + 1) * H].rearrange("p (u t) -> p u t", t=4),
                turned[m][:].rearrange("p t u -> p u t"),
                ACT.Square,
            )

        def quantise(j):
            nc.vector.quantize_mx(
                out=hq[j][:].bitcast(FP8X4), scales=hqs[:, 2 * j * P : 2 * (j + 1) * P], in_=hb[j][:]
            )

        def products(j, c, bank):
            acc = psum.tile([P, 2, P], F32, name="acc%d_%d" % (j, c), tag=bank)
            for b in range(2):
                m = 2 * j + b
                nc.tensor.matmul_mx(
                    out=acc[:, b, :],
                    lhsT=w2g[m][:, c * P : (c + 1) * P].bitcast(FP8X4),
                    lhsT_scale=w2gs[m][:, c * P : (c + 1) * P],
                    rhs=hq[j][:, b * P : (b + 1) * P].bitcast(FP8X4),
                    rhs_scale=hqs[:, m * P : (m + 1) * P],
                    start=True,
                    stop=True,
                )
            return acc[:].rearrange("p b u -> p (b u)")

        def leave(name, acc):
            dst = kept(name, [P, 2 * P], F32)
            nc.scalar.copy(dst[:], acc)
            return dst

        def gates(j):
            return g[:, 2 * j * P : 2 * (j + 1) * P]

        def gated(name, j, acc):
            dst = kept(name, [P, 2 * P], F32)
            nc.vector.tensor_tensor(dst[:], acc, gates(j), MULT)
            return dst

        def window(c, j):
            return res[c][:].indirect(entries(tok, 2 * j * P, 2 * (j + 1) * P))

        for m in (0, 1):
            gather_w1(m, m + 1, kept("w1g%d" % m, [P, H], U32))
        xg = gather(kept("xg_first", [P, 2 * P], U32), x_window, tok, P, 0, 2)
        xg.extend(gather(kept("xg_rest", [P, 4 * P], U32), x_window, tok, P, 2, B))
        gather_w1(2, 3, placed("w1g2", [P, H], U32, ROWS_AT - 1536))
        gather_w1(3, 4, placed("w1g3", [P, H], U32, ROWS_AT + 512))
        gather_w1(4, 6, placed("w1g45", [P, 2 * H], U32, ROWS_AT + 2560))
        for m in range(3):
            first_layer(m, "ABC"[m])
        turn(0, "D")
        turn(1, "E")
        square(0)
        square(1)
        first_layer(3, "B")
        turn(2, "D")
        first_layer(4, "E")
        square(2)
        w2g = gather(kept("w2g", [P, B * N], U32), w2_window, col2, N, 0, B)
        quantise(0)
        w2gs = gather(kept("w2gs_first", [P, 2 * N], U8), w2s[:], col2, N, 0, 2)
        w2gs.extend(gather(kept("w2gs_rest", [P, 4 * N], U8), w2s[:], col2, N, 2, B))
        first_layer(5, "B")
        turn(3, "A")
        square(3)
        acc00 = products(0, 0, "F")
        acc01 = products(0, 1, "G")
        y01 = gated("y01", 0, acc01)
        quantise(1)
        y00 = leave("y00", acc00)
        nc.vector.tensor_tensor(window(0, 0), y00[:], gates(0), MULT)
        turn(4, "H")
        turn(5, "C")
        square(4)
        square(5)
        acc10 = products(1, 0, "B")
        acc11 = products(1, 1, "D")
        y11 = gated("y11", 1, acc11)
        quantise(2)
        y10 = leave("y10", acc10)
        nc.scalar.activation(window(1, 0), y01[:], ACT.Copy)
        nc.vector.tensor_tensor(window(0, 1), y10[:], gates(1), MULT)
        y20 = gated("y20", 2, products(2, 0, "A"))
        y21 = gated("y21", 2, products(2, 1, "E"))
        nc.scalar.activation(window(1, 1), y11[:], ACT.Copy)
        nc.scalar.activation(window(1, 2), y21[:], ACT.Copy)
        nc.sync.dma_start(out=out[P:, :], in_=res[1][:])
        nc.vector.tensor_copy(window(0, 2), y20[:])
        nc.sync.dma_start(out=out[:P, :], in_=res[0][:])
